import numpy as np
import ml_dtypes


def mxq(x, axis, fmt="e4m3"):
    dtype, down = {"e4m3": (ml_dtypes.float8_e4m3fn, 7), "e5m2": (ml_dtypes.float8_e5m2, 14)}[fmt]
    v = np.moveaxis(np.asarray(x, np.float32).astype(ml_dtypes.bfloat16).astype(np.float64), axis, -1)
    blocks = v.reshape(v.shape[:-1] + (-1, 32))
    amax = np.abs(blocks).max(-1, keepdims=True)
    byte = np.maximum(np.where(amax > 0, np.frexp(amax)[1] - 1 + 127, 0) - down, 1)
    scale = np.exp2(byte - 127.0)
    codes = (blocks / scale).astype(np.float32).astype(dtype).astype(np.float64)
    return np.moveaxis((codes * scale).reshape(v.shape), -1, axis)


WIDE = False


def mx_kscale(k):
    if not WIDE:
        return np.ones(k)
    levels = np.array([10, -10, 5, -5, 0])
    if k % 512:
        return np.exp2(np.random.permutation(np.resize(levels, k // 32))).repeat(32)
    a = np.empty((k // 512, 16))
    for p in range(k // 512):
        a[p, :8] = np.random.permutation(np.resize(levels, 8))
        for g in range(8):
            far = levels[np.abs(levels - a[p, g]) >= 10]
            a[p, g + 8] = far[np.random.randint(len(far))]
    return np.exp2(a.ravel()).repeat(32)


def f64(x):
    return np.asarray(x).astype(np.float64)


def striped(idx):
    return np.tile(np.asarray(idx).reshape(-1, 16).T, (8, 1)).astype(np.uint16)


def unstriped(offs):
    return offs[:16].T.reshape(-1).astype(np.int64)


E2M1 = np.array([0.0, 0.5, 1.0, 1.5, 2.0, 3.0, 4.0, 6.0, -0.0, -0.5, -1.0, -1.5, -2.0, -3.0, -4.0, -6.0])


def pack_weight(w, fmt):
    k, n = w.shape
    w = f64(np.asarray(w, np.float32).astype(ml_dtypes.bfloat16)).reshape(k // 32, 32, n)
    amax = np.abs(w).max(1)
    if fmt == "e4m3":
        byte = np.frexp(amax)[1] - 1 + 127 - 7
    else:
        mant, ex = np.frexp(amax / 6.0)
        byte = np.where(mant > 0.5, ex, ex - 1) + 127
    byte = np.clip(np.where(amax > 0, byte, 1), 1, 254)
    scaled = (w * np.exp2(127.0 - byte)[:, None, :]).reshape(k, n).astype(np.float32)
    by_word = np.ascontiguousarray(scaled.reshape(k // 512, 128, 4, n).transpose(0, 1, 3, 2))
    if fmt == "e4m3":
        words = by_word.astype(ml_dtypes.float8_e4m3fn).view(np.uint8)
    else:
        c = by_word.astype(ml_dtypes.float4_e2m1fn).view(np.uint8) & 0xF
        words = (c[..., 0::2] | (c[..., 1::2] << 4)).reshape(k // 512, 128, 2 * n)
    return np.ascontiguousarray(words), np.ascontiguousarray(byte.astype(np.uint8).reshape(k // 512, 16, n))


def unpack_weight(words, scales, fmt):
    g, _, n = scales.shape
    words = np.ascontiguousarray(words).reshape(g, 128, n, -1)
    if fmt == "e4m3":
        vals = words.view(ml_dtypes.float8_e4m3fn).astype(np.float64)
    else:
        nib = np.empty((g, 128, n, 4), np.uint8)
        nib[..., 0::2] = words & 0xF
        nib[..., 1::2] = words >> 4
        vals = E2M1[nib]
    vals = vals * np.repeat(np.exp2(scales.astype(np.float64) - 127.0), 8, axis=1)[..., None]
    return vals.transpose(0, 1, 3, 2).reshape(g * 512, n)


def sigmoid(v):
    return 1.0 / (1.0 + np.exp(-v))


def bf(x):
    return np.asarray(x, np.float32).astype(ml_dtypes.bfloat16)


def planes(Y):
    r, m = Y.shape
    b = f64(bf(Y)).reshape(r // 32, 32, m)
    amax = np.abs(b).max(1)
    byte = np.clip(np.where(amax > 0, np.frexp(amax)[1] - 1 + 127 - 7, 1), 1, 254)
    codes = (b * np.exp2(127.0 - byte)[:, None, :]).reshape(r, m).astype(np.float32).astype(ml_dtypes.float8_e4m3fn).view(np.uint8)
    words = codes.reshape(r // 512, 128, 4, m).transpose(0, 1, 3, 2)
    return np.ascontiguousarray(words), np.ascontiguousarray(byte.astype(np.uint8).reshape(r // 512, 16, m))


D, T, I, Q, E, H = 512, 2048, 512, 256, 512, 32


def setup_inputs():
    n = np.random.standard_normal
    idx = np.random.permutation(T)[:I]
    fd = mx_kscale(D)
    fi = mx_kscale(I)
    keysp = pack_weight(n((D, T)) / fd[:, None], "e2m1")
    return {
        "query": (n((D, Q)) * 1.2 / np.sqrt(D) * fd[:, None]).astype(np.float32),
        "keys_words": keysp[0],
        "keys_scales": keysp[1],
        "guess": np.tile(np.random.uniform(0.05, 0.3, T), (128, 1)).astype(np.float32),
        "steep": np.tile(np.random.uniform(1.0, 3.0, T), (128, 1)).astype(np.float32),
        "thr": np.tile(np.random.uniform(-0.5, 1.0, T), (128, 1)).astype(np.float32),
        "lam": (np.random.uniform(0.6, 1.5, (Q, 1))).astype(np.float32),
        "eager": (np.random.uniform(0.8, 2.0, (Q, 1))).astype(np.float32),
        "thresh": (np.random.uniform(1.5, 4.0, (Q, 1))).astype(np.float32),
        "os": (np.random.uniform(4.0, 16.0, (1, I)) * fi).astype(np.float32),
        "vals": (n((E, T))).astype(np.float32),
        "vsc": (np.random.uniform(0.5, 2.0, (1, I)) / fi).astype(np.float32),
        "offs": striped(idx),
    }


def reference(query, keys_words, keys_scales, guess, steep, thr, lam, eager, thresh, os, vals, vsc, offs):
    idx = unstriped(offs)
    keysu = unpack_weight(keys_words, keys_scales, "e2m1")
    queryq = mxq(f64(query), 0, "e4m3")
    keysidxg = keysu[:, idx]
    a = queryq.T @ keysidxg
    sg = sigmoid((a - f64(thr)[:1][:, idx]) * f64(steep)[:1][:, idx])
    s = np.log(sg * (1.0 - f64(guess)[:1][:, idx]) + f64(guess)[:1][:, idx]) * f64(lam)
    m0 = np.max(s, axis=1, keepdims=True)
    m1 = np.mean(s, axis=1, keepdims=True)
    p = np.exp(s - m0)
    gt0 = sigmoid((m0 - m1) * f64(eager) - f64(thresh))
    w = p / np.sum(p, axis=1, keepdims=True) * gt0
    wo1 = w * f64(os)
    wt1 = wo1.T
    vg = f64(vals)[:, idx].reshape(E, H, I // H).mean(axis=2)
    vgr = np.repeat(vg, I // H, axis=1)
    vd = (f64(vals)[:, idx] - vgr) * f64(vsc)
    vt1 = vd.T
    vt1q = mxq(vt1, 0, "e4m3")
    wt1q = mxq(wt1, 0, "e4m3")
    o = vt1q.T @ wt1q
    words, scales = planes(o)
    return o, words, scales

@@ -1,0 +1,408 @@
+from contextlib import ExitStack
+
+import concourse.mybir as mybir
+from concourse.masks import make_identity
+
+D, T, I, Q, E = 512, 2048, 512, 256, 512
+FLOPS = 2 * D * I * Q + 2 * I * E * Q
+
+F32 = mybir.dt.float32
+BF16 = mybir.dt.bfloat16
+I32 = mybir.dt.int32
+U32 = mybir.dt.uint32
+U16 = mybir.dt.uint16
+U8 = mybir.dt.uint8
+FP8X4 = mybir.dt.float8_e4m3fn_x4
+FP4X4 = mybir.dt.float4_e2m1fn_x4
+ALU = mybir.AluOpType
+ACT = mybir.ActivationFunctionType
+AX = mybir.AxisListType
+
+P = 128
+PACK = 4
+STRETCH = 16
+H = I // STRETCH
+QT = Q // P
+ROW = P - 1
+
+
+def tile_attend_answerodds_abstaining_centredvalues_pl_kernel(
+    tc, query, keys_words, keys_scales, guess, steep, thr, lam, eager, thresh, slot_os, vals, vsc, offs,
+    out_0, out_1, out_2,
+):
+    nc = tc.nc
+    with ExitStack() as ctx:
+        sb = ctx.enter_context(tc.tile_pool(name="sb", bufs=1))
+        ps = ctx.enter_context(tc.psum_pool(name="ps", bufs=1))
+
+        def held(shape, dtype, name):
+            return sb.tile(shape, dtype, name=name, align_bytes=64)
+
+        def bank(shape, b, name):
+            return ps.tile(shape, F32, name=name, tag="bank%d" % b)
+
+        offs_t = sb.tile([P, I // 16], U16, name="offs_t")
+        kw_pool = held([P, T], U16, "kw_pool")
+        ks_pool = held([P, T], U8, "ks_pool")
+        thr_pool = held([P, T], F32, "thr_pool")
+        steep_pool = held([P, T], F32, "steep_pool")
+        guess_pool = held([P, T], F32, "guess_pool")
+        q_raw = held([P, PACK, Q], F32, "q_raw")
+        v_pool = [held([P, T], F32, "v_pool%d" % t) for t in range(PACK)]
+        lam_t = held([P, QT], F32, "lam_t")
+        eager_t = held([P, QT], F32, "eager_t")
+        thresh_t = held([P, QT], F32, "thresh_t")
+        os_t = held([P, PACK], F32, "os_t")
+        vsc_t = held([P, PACK], F32, "vsc_t")
+        ident = held([P, P], F32, "ident")
+
+        nc.vector.memset(ks_pool[:].bitcast(I32), 0)
+        nc.vector.memset(thr_pool[0:ROW, :], 0.0)
+        nc.vector.memset(steep_pool[0:ROW, :], 0.0)
+        make_identity(nc, ident[:])
+        nc.gpsimd.memset(guess_pool[0:ROW, :], 0.0)
+
+        def row_numbers(queue, dst, src):
+            with nc.allow_non_contiguous_dma(reason="one number a query row"):
+                queue.dma_start(dst[:], src[:, 0].rearrange("(u p) -> p u", p=P))
+
+        def key_scale_rows(queue, g):
+            queue.dma_start(
+                ks_pool[32 * g : 32 * g + 4, :].bitcast(I32), keys_scales[0, 4 * g : 4 * g + 4, :].bitcast(I32)
+            )
+
+        def token_columns(row, b, name):
+            turned = bank([P, 4, P], b, name + "_turned")
+            for j in range(4):
+                nc.tensor.transpose(turned[:, j, :], row[:, j * P : (j + 1) * P], ident[:])
+            return turned[:, :, ROW]
+
+        v_rows = vals.rearrange("(p t) n -> t p n", t=PACK)
+        out_rows = out_0.rearrange("(p t) q -> p t q", t=PACK)
+        v_codes = [held([P, P], U32, "v_codes%d" % t) for t in range(PACK)]
+        v_scales = [held([P, P], U8, "v_scales%d" % t) for t in range(PACK)]
+        o_bf = held([P, Q, PACK], BF16, "o_bf")
+        o_codes = held([P, Q], U32, "o_codes")
+        o_scales = held([P, Q], U8, "o_scales")
+        nc.sync.dma_start(offs_t[:], offs)
+        nc.scalar.dma_start(thr_pool[ROW:P, :], thr[0:1, :])
+        nc.sync.dma_start(kw_pool[:].bitcast(I32), keys_words[0].bitcast(I32))
+        nc.scalar.dma_start(steep_pool[ROW:P, :], steep[0:1, :])
+        key_scale_rows(nc.sync, 0)
+        key_scale_rows(nc.sync, 1)
+        key_scale_rows(nc.sync, 2)
+        key_scale_rows(nc.sync, 3)
+        nc.sync.dma_start(q_raw[:], query.rearrange("(p j) q -> p j q", j=PACK))
+        nc.sync.dma_start(v_pool[0][:], v_rows[0])
+        nc.sync.dma_start(guess_pool[ROW:P, :], guess[0:1, :])
+        nc.sync.dma_start(vsc_t[:], vsc[0].rearrange("(s r) -> s r", r=PACK))
+        nc.sync.dma_start(v_pool[1][:], v_rows[1])
+        row_numbers(nc.sync, lam_t, lam)
+        nc.sync.dma_start(v_pool[2][:], v_rows[2])
+        row_numbers(nc.sync, eager_t, eager)
+        row_numbers(nc.sync, thresh_t, thresh)
+        nc.sync.dma_start(os_t[:], slot_os[0].rearrange("(s r) -> s r", r=PACK))
+        nc.sync.dma_start(v_pool[3][:], v_rows[3])
+
+        kw = held([P, I], U16, "kw")
+        nc.vector.tensor_copy(kw[:], kw_pool[:].indirect(offs_t[:]))
+
+        ks = held([P, I], U8, "ks")
+        nc.vector.tensor_copy(ks[:], ks_pool[:].indirect(offs_t[:]))
+
+        thr_row = held([P, I], F32, "thr_row")
+        nc.scalar.activation(thr_row[:], thr_pool[:].indirect(offs_t[:]), ACT.Copy)
+
+        thr_col = token_columns(thr_row, 4, "thr")
+
+        neg_thr = held([P, 4], F32, "neg_thr")
+        nc.vector.tensor_scalar(neg_thr[:], thr_col, -1.0, None, ALU.mult)
+
+        steep_row = held([P, I], F32, "steep_row")
+        nc.scalar.activation(steep_row[:], steep_pool[:].indirect(offs_t[:]), ACT.Copy)
+
+        steep_col = token_columns(steep_row, 5, "steep")
+
+        steep_c = held([P, 4], F32, "steep_c")
+        shift_c = held([P, 4], F32, "shift_c")
+        nc.vector.tensor_tensor(shift_c[:], steep_col, neg_thr[:], ALU.mult)
+        nc.vector.tensor_copy(steep_c[:], steep_col)
+
+        q_bf = held([P, Q, PACK], BF16, "q_bf")
+        nc.vector.tensor_copy(q_bf[:], q_raw[:].rearrange("p j q -> p q j"))
+
+        q_codes = held([P, Q], U32, "q_codes")
+        q_scales = held([P, Q], U8, "q_scales")
+        nc.vector.quantize_mx(out=q_codes[:].bitcast(FP8X4), scales=q_scales[:], in_=q_bf[:].rearrange("p q j -> p (q j)"))
+
+        a_ps = [bank([P, Q], b, "a_ps%d" % b) for b in (0, 1, 2, 3)]
+        for j in range(4):
+            nc.tensor.matmul_mx(
+                out=a_ps[j][:],
+                lhsT=kw[:, j * P : (j + 1) * P].bitcast(FP4X4),
+                lhsT_scale=ks[:, j * P : (j + 1) * P],
+                rhs=q_codes[:].bitcast(FP8X4),
+                rhs_scale=q_scales[:],
+                start=True,
+                stop=True,
+            )
+
+        guess_row = held([P, I], F32, "guess_row")
+        nc.scalar.activation(guess_row[:], guess_pool[:].indirect(offs_t[:]), ACT.Copy)
+
+        guess_col = token_columns(guess_row, 4, "guess")
+
+        guess_c = held([P, 4], F32, "guess_c")
+        rest_c = held([P, 4], F32, "rest_c")
+        nc.vector.tensor_copy(guess_c[:], guess_col)
+        nc.vector.tensor_scalar(rest_c[:], guess_col, -1.0, 1.0, ALU.mult, ALU.add)
+
+        sg = [held([P, Q], F32, "sg%d" % j) for j in range(4)]
+        for j in range(4):
+            nc.scalar.activation(
+                sg[j][:], a_ps[j][:], ACT.Sigmoid, bias=shift_c[:, j : j + 1], scale=steep_c[:, j : j + 1]
+            )
+
+        chance = [held([P, Q], F32, "chance%d" % j) for j in range(4)]
+        for j in range(4):
+            nc.vector.tensor_scalar(
+                chance[j][:], sg[j][:], rest_c[:, j : j + 1], guess_c[:, j : j + 1], ALU.mult, ALU.add
+            )
+        chance_q = [bank([P, I], b, "chance_q%d" % b) for b in (4, 5)]
+        for j in range(4):
+            for u in range(QT):
+                nc.tensor.transpose(chance_q[u][:, j * P : (j + 1) * P], chance[j][:, u * P : (u + 1) * P], ident[:])
+
+        ln_q = [held([P, PACK, P], F32, "ln_q%d" % u) for u in range(QT)]
+        ln_sum = [held([P, 1], F32, "ln_sum%d" % u) for u in range(QT)]
+        for u in range(QT):
+            nc.scalar.activation(
+                ln_q[u][:], chance_q[u][:].rearrange("q (s r) -> q r s", r=PACK), ACT.Ln, accum_out=ln_sum[u][:]
+            )
+
+        neg_lam = held([P, QT], F32, "neg_lam")
+        lam_mean = held([P, QT], F32, "lam_mean")
+        nc.vector.tensor_scalar(neg_lam[:], lam_t[:], -1.0, None, ALU.mult)
+        nc.vector.tensor_scalar(lam_mean[:], lam_t[:], 1.0 / I, None, ALU.mult)
+
+        neg_s = [held([P, PACK, P], F32, "neg_s%d" % u) for u in range(QT)]
+        neg_m0 = [held([P, 1], F32, "neg_m0_%d" % u) for u in range(QT)]
+        lag = held([P, QT], F32, "lag")
+        for u in range(QT):
+            nc.vector.tensor_scalar(
+                neg_s[u][:], ln_q[u][:], neg_lam[:, u : u + 1], None, ALU.mult, ALU.min, accum_out=neg_m0[u][:]
+            )
+        for u in range(QT):
+            nc.vector.tensor_scalar(
+                lag[:, u : u + 1], ln_sum[u][:], lam_mean[:, u : u + 1], neg_m0[u][:], ALU.mult, ALU.add
+            )
+
+        odds = held([P, QT], F32, "odds")
+        for u in range(QT):
+            nc.scalar.activation(
+                odds[:, u : u + 1], lag[:, u : u + 1], ACT.Exp, bias=thresh_t[:, u : u + 1], scale=eager_t[:, u : u + 1]
+            )
+
+        odds1 = held([P, QT], F32, "odds1")
+        gate = held([P, QT], F32, "gate")
+        nc.vector.tensor_scalar(odds1[:], odds[:], 1.0, None, ALU.add)
+        nc.vector.reciprocal(gate[:], odds1[:])
+
+        p_t = [held([P, I], F32, "p_t%d" % u) for u in range(QT)]
+        p_sum = [held([P, 1], F32, "p_sum%d" % u) for u in range(QT)]
+        for u in range(QT):
+            nc.scalar.activation(
+                p_t[u][:], neg_s[u][:].rearrange("q r s -> q (r s)"), ACT.Exp,
+                bias=neg_m0[u][:], scale=-1.0, accum_out=p_sum[u][:],
+            )
+
+        inv_sum0 = held([P, 1], F32, "inv_sum0")
+        nc.vector.reciprocal(inv_sum0[:], p_sum[0][:])
+        w_t0 = held([P, I], F32, "w_t0")
+        nc.vector.tensor_scalar(w_t0[:], p_t[0][:], inv_sum0[:], gate[:, 0 : 1], ALU.mult, ALU.mult)
+        w_turned0 = bank([P, PACK, P], 0, "w_turned0")
+        for r in range(PACK):
+            nc.tensor.transpose(w_turned0[:, r, :], w_t0[:, r * P : (r + 1) * P], ident[:])
+
+        inv_sum1 = held([P, 1], F32, "inv_sum1")
+        nc.vector.reciprocal(inv_sum1[:], p_sum[1][:])
+        w_t1 = held([P, I], F32, "w_t1")
+        nc.vector.tensor_scalar(w_t1[:], p_t[1][:], inv_sum1[:], gate[:, 1 : 2], ALU.mult, ALU.mult)
+        w_turned1 = bank([P, PACK, P], 1, "w_turned1")
+        for r in range(PACK):
+            nc.tensor.transpose(w_turned1[:, r, :], w_t1[:, r * P : (r + 1) * P], ident[:])
+
+        w_bf0 = held([P, P, PACK], BF16, "w_bf0")
+        nc.vector.tensor_tensor(
+            w_bf0[:], w_turned0[:].rearrange("s r q -> s q r"), os_t[:].unsqueeze(1).to_broadcast([P, P, PACK]), ALU.mult
+        )
+
+        w_bf1 = held([P, P, PACK], BF16, "w_bf1")
+        nc.vector.tensor_tensor(
+            w_bf1[:], w_turned1[:].rearrange("s r q -> s q r"), os_t[:].unsqueeze(1).to_broadcast([P, P, PACK]), ALU.mult
+        )
+
+        w_codes0 = held([P, P], U32, "w_codes0")
+        w_scales0 = held([P, P], U8, "w_scales0")
+        nc.vector.quantize_mx(out=w_codes0[:].bitcast(FP8X4), scales=w_scales0[:], in_=w_bf0[:].rearrange("s q r -> s (q r)"))
+
+        w_codes1 = held([P, P], U32, "w_codes1")
+        w_scales1 = held([P, P], U8, "w_scales1")
+        nc.vector.quantize_mx(out=w_codes1[:].bitcast(FP8X4), scales=w_scales1[:], in_=w_bf1[:].rearrange("s q r -> s (q r)"))
+
+        picked0 = held([P, I], F32, "picked0")
+        nc.scalar.activation(picked0[:], v_pool[0][:].indirect(offs_t[:]), ACT.Copy)
+        v_turned0 = bank([P, PACK, P], 6, "v_turned0")
+        for r in range(PACK):
+            nc.tensor.matmul(
+                v_turned0[:, r, :], picked0[:, r:I:PACK], ident[:], start=(r == 0), stop=False, is_transpose=True
+            )
+        sums0 = held([P, H], F32, "sums0")
+        nc.vector.tensor_reduce(sums0[:], picked0[:].rearrange("p (h k) -> p h k", k=STRETCH), AX.X, ALU.add)
+        neg_mean0 = held([P, H, STRETCH // PACK], F32, "neg_mean0")
+        nc.vector.tensor_scalar(neg_mean0[:], sums0[:].unsqueeze(2).to_broadcast([P, H, STRETCH // PACK]), -1.0 / STRETCH, None, ALU.mult)
+        for r in range(PACK):
+            nc.tensor.matmul(
+                v_turned0[:, r, :], neg_mean0[:].rearrange("p h u -> p (h u)"), ident[:], start=False, stop=(r == PACK - 1), is_transpose=True
+            )
+        v_bf0 = held([P, P, PACK], BF16, "v_bf0")
+        nc.vector.tensor_tensor(
+            v_bf0[:], v_turned0[:].rearrange("s r e -> s e r"), vsc_t[:].unsqueeze(1).to_broadcast([P, P, PACK]), ALU.mult
+        )
+        nc.vector.quantize_mx(out=v_codes[0][:].bitcast(FP8X4), scales=v_scales[0][:], in_=v_bf0[:].rearrange("s e r -> s (e r)"))
+
+        picked1 = held([P, I], F32, "picked1")
+        nc.vector.tensor_copy(picked1[:].rearrange("p (r s) -> p s r", r=PACK), v_pool[1][:].indirect(offs_t[:]))
+        v_turned1 = bank([P, PACK, P], 7, "v_turned1")
+        for r in range(PACK):
+            nc.tensor.matmul(
+                v_turned1[:, r, :], picked1[:, r * P : (r + 1) * P], ident[:], start=(r == 0), stop=False, is_transpose=True
+            )
+        sums1 = held([P, H], F32, "sums1")
+        nc.vector.tensor_reduce(sums1[:], picked1[:].rearrange("p (r h u) -> p h r u", r=PACK, h=H), AX.XY, ALU.add)
+        neg_mean1 = held([P, H, STRETCH // PACK], F32, "neg_mean1")
+        nc.vector.tensor_scalar(neg_mean1[:], sums1[:].unsqueeze(2).to_broadcast([P, H, STRETCH // PACK]), -1.0 / STRETCH, None, ALU.mult)
+        for r in range(PACK):
+            nc.tensor.matmul(
+                v_turned1[:, r, :], neg_mean1[:].rearrange("p h u -> p (h u)"), ident[:], start=False, stop=(r == PACK - 1), is_transpose=True
+            )
+        v_bf1 = held([P, P, PACK], BF16, "v_bf1")
+        nc.vector.tensor_tensor(
+            v_bf1[:], v_turned1[:].rearrange("s r e -> s e r"), vsc_t[:].unsqueeze(1).to_broadcast([P, P, PACK]), ALU.mult
+        )
+        nc.vector.quantize_mx(out=v_codes[1][:].bitcast(FP8X4), scales=v_scales[1][:], in_=v_bf1[:].rearrange("s e r -> s (e r)"))
+
+        picked2 = held([P, I], F32, "picked2")
+        nc.scalar.activation(picked2[:], v_pool[2][:].indirect(offs_t[:]), ACT.Copy)
+        v_turned2 = bank([P, PACK, P], 6, "v_turned2")
+        for r in range(PACK):
+            nc.tensor.matmul(
+                v_turned2[:, r, :], picked2[:, r:I:PACK], ident[:], start=(r == 0), stop=False, is_transpose=True
+            )
+        sums2 = held([P, H], F32, "sums2")
+        nc.vector.tensor_reduce(sums2[:], picked2[:].rearrange("p (h k) -> p h k", k=STRETCH), AX.X, ALU.add)
+        neg_mean2 = held([P, H, STRETCH // PACK], F32, "neg_mean2")
+        nc.vector.tensor_scalar(neg_mean2[:], sums2[:].unsqueeze(2).to_broadcast([P, H, STRETCH // PACK]), -1.0 / STRETCH, None, ALU.mult)
+        for r in range(PACK):
+            nc.tensor.matmul(
+                v_turned2[:, r, :], neg_mean2[:].rearrange("p h u -> p (h u)"), ident[:], start=False, stop=(r == PACK - 1), is_transpose=True
+            )
+        v_bf2 = held([P, P, PACK], BF16, "v_bf2")
+        nc.vector.tensor_tensor(
+            v_bf2[:], v_turned2[:].rearrange("s r e -> s e r"), vsc_t[:].unsqueeze(1).to_broadcast([P, P, PACK]), ALU.mult
+        )
+        nc.vector.quantize_mx(out=v_codes[2][:].bitcast(FP8X4), scales=v_scales[2][:], in_=v_bf2[:].rearrange("s e r -> s (e r)"))
+
+        picked3 = held([P, I], F32, "picked3")
+        nc.scalar.activation(picked3[:], v_pool[3][:].indirect(offs_t[:]), ACT.Copy)
+        v_turned3 = bank([P, PACK, P], 7, "v_turned3")
+        for r in range(PACK):
+            nc.tensor.matmul(
+                v_turned3[:, r, :], picked3[:, r:I:PACK], ident[:], start=(r == 0), stop=False, is_transpose=True
+            )
+        sums3 = held([P, H], F32, "sums3")
+        nc.vector.tensor_reduce(sums3[:], picked3[:].rearrange("p (h k) -> p h k", k=STRETCH), AX.X, ALU.add)
+        neg_mean3 = held([P, H, STRETCH // PACK], F32, "neg_mean3")
+        nc.vector.tensor_scalar(neg_mean3[:], sums3[:].unsqueeze(2).to_broadcast([P, H, STRETCH // PACK]), -1.0 / STRETCH, None, ALU.mult)
+        for r in range(PACK):
+            nc.tensor.matmul(
+                v_turned3[:, r, :], neg_mean3[:].rearrange("p h u -> p (h u)"), ident[:], start=False, stop=(r == PACK - 1), is_transpose=True
+            )
+        v_bf3 = held([P, P, PACK], BF16, "v_bf3")
+        nc.vector.tensor_tensor(
+            v_bf3[:], v_turned3[:].rearrange("s r e -> s e r"), vsc_t[:].unsqueeze(1).to_broadcast([P, P, PACK]), ALU.mult
+        )
+        nc.vector.quantize_mx(out=v_codes[3][:].bitcast(FP8X4), scales=v_scales[3][:], in_=v_bf3[:].rearrange("s e r -> s (e r)"))
+
+        o_sb0 = held([P, PACK, P], F32, "o_sb0")
+        o_ps = bank([P, 2, P], 2, "o_ps0_0")
+        for k in range(2):
+            nc.tensor.matmul_mx(
+                out=o_ps[:, k, :],
+                lhsT=v_codes[0 + k][:].bitcast(FP8X4),
+                lhsT_scale=v_scales[0 + k][:],
+                rhs=w_codes0[:].bitcast(FP8X4),
+                rhs_scale=w_scales0[:],
+                start=True,
+                stop=True,
+            )
+        nc.scalar.copy(o_sb0[:, 0 : 2, :], o_ps[:])
+        o_ps = bank([P, 2, P], 3, "o_ps0_1")
+        for k in range(2):
+            nc.tensor.matmul_mx(
+                out=o_ps[:, k, :],
+                lhsT=v_codes[2 + k][:].bitcast(FP8X4),
+                lhsT_scale=v_scales[2 + k][:],
+                rhs=w_codes0[:].bitcast(FP8X4),
+                rhs_scale=w_scales0[:],
+                start=True,
+                stop=True,
+            )
+        nc.scalar.copy(o_sb0[:, 2 : 4, :], o_ps[:])
+        nc.sync.dma_start(out_rows[:, :, 0 : 128], o_sb0[:])
+
+        o_sb1 = held([P, PACK, P], F32, "o_sb1")
+        o_ps = bank([P, 2, P], 4, "o_ps1_0")
+        for k in range(2):
+            nc.tensor.matmul_mx(
+                out=o_ps[:, k, :],
+                lhsT=v_codes[0 + k][:].bitcast(FP8X4),
+                lhsT_scale=v_scales[0 + k][:],
+                rhs=w_codes1[:].bitcast(FP8X4),
+                rhs_scale=w_scales1[:],
+                start=True,
+                stop=True,
+            )
+        nc.vector.tensor_copy(o_sb1[:, 0 : 2, :], o_ps[:])
+        o_ps = bank([P, 2, P], 5, "o_ps1_1")
+        for k in range(2):
+            nc.tensor.matmul_mx(
+                out=o_ps[:, k, :],
+                lhsT=v_codes[2 + k][:].bitcast(FP8X4),
+                lhsT_scale=v_scales[2 + k][:],
+                rhs=w_codes1[:].bitcast(FP8X4),
+                rhs_scale=w_scales1[:],
+                start=True,
+                stop=True,
+            )
+        nc.scalar.copy(o_sb1[:, 2 : 4, :], o_ps[:])
+        nc.sync.dma_start(out_rows[:, :, 128 : 256], o_sb1[:])
+
+        nc.vector.tensor_copy(o_bf[:, 0 : 128, :], o_sb0[:].rearrange("p t q -> p q t"))
+
+        nc.vector.tensor_copy(o_bf[:, 128 : 256, :], o_sb1[:].rearrange("p t q -> p q t"))
+
+        nc.vector.quantize_mx(
+            out=o_codes[:, 0 : 128].bitcast(FP8X4), scales=o_scales[:, 0 : 128],
+            in_=o_bf[:, 0 : 128, :].rearrange("p q t -> p (q t)"),
+        )
+
+        nc.vector.quantize_mx(
+            out=o_codes[:, 128 : 256].bitcast(FP8X4), scales=o_scales[:, 128 : 256],
+            in_=o_bf[:, 128 : 256, :].rearrange("p q t -> p (q t)"),
+        )
+
+        nc.sync.dma_start(out_1[0].rearrange("p q r -> p (q r)").bitcast(I32), o_codes[:].bitcast(I32))
+        for g in range(4):
+            queue = nc.scalar if g % 2 == 0 else nc.sync
+            queue.dma_start(out_2[0, 4 * g : 4 * g + 4, :].bitcast(I32), o_scales[32 * g : 32 * g + 4, :].bitcast(I32))

@@ -1,7 +1,6 @@
 from contextlib import ExitStack
 
 import concourse.mybir as mybir
-from concourse.masks import make_identity
 
 D, T, I, Q, E = 512, 2048, 512, 256, 512
 FLOPS = 2 * D * I * Q + 2 * I * E * Q
@@ -20,10 +19,33 @@ AX = mybir.AxisListType
 
 P = 128
 PACK = 4
+QUAD = 32
 STRETCH = 16
 H = I // STRETCH
 QT = Q // P
 ROW = P - 1
+PLACES = {
+    "v_pool1": 0,
+    "ln_q0": 0,
+    "ln_q1": 2048,
+    "v_pool3": 8192,
+    "p_t0": 8192,
+    "p_t1": 10240,
+    "odds": 12288,
+    "v_pool2": 16384,
+    "neg_s0": 16384,
+    "neg_s1": 18432,
+    "v0_codes": 20480,
+    "v_pool0": 24576,
+    "neg_lam": 24576,
+    "lam_mean": 24704,
+    "sums1": 32768,
+    "v_bf0": 32768,
+    "v_bf1": 2048,
+    "sums3": 33792,
+    "v_bf2": 33792,
+    "v_bf3": 8192
+}
 
 
 def tile_attend_answerodds_abstaining_centredvalues_pl_kernel(
@@ -33,13 +55,22 @@ def tile_attend_answerodds_abstaining_centredvalues_pl_kernel(
     nc = tc.nc
     with ExitStack() as ctx:
         sb = ctx.enter_context(tc.tile_pool(name="sb", bufs=1))
+        shared = ctx.enter_context(tc.tile_pool(name="shared", bufs=1))
         ps = ctx.enter_context(tc.psum_pool(name="ps", bufs=1))
 
-        def held(shape, dtype, name):
+        def held(shape, dtype, name, tag=None):
+            if name in PLACES:
+                return shared.tile(shape, dtype, name=name, align_bytes=64, offset=PLACES[name])
             return sb.tile(shape, dtype, name=name, align_bytes=64)
 
         def bank(shape, b, name):
             return ps.tile(shape, F32, name=name, tag="bank%d" % b)
+
+        def quantise(bf, width, name):
+            codes = held([P, width], U32, name + "_codes")
+            scales = held([P, width], U8, name + "_scales")
+            nc.vector.quantize_mx(out=codes[:].bitcast(FP8X4), scales=scales[:], in_=bf)
+            return codes, scales
 
         offs_t = sb.tile([P, I // 16], U16, name="offs_t")
         kw_pool = held([P, T], U16, "kw_pool")
@@ -54,88 +85,123 @@ def tile_attend_answerodds_abstaining_centredvalues_pl_kernel(
         thresh_t = held([P, QT], F32, "thresh_t")
         os_t = held([P, PACK], F32, "os_t")
         vsc_t = held([P, PACK], F32, "vsc_t")
-        ident = held([P, P], F32, "ident")
 
-        nc.vector.memset(ks_pool[:].bitcast(I32), 0)
-        nc.vector.memset(thr_pool[0:ROW, :], 0.0)
-        nc.vector.memset(steep_pool[0:ROW, :], 0.0)
-        make_identity(nc, ident[:])
-        nc.gpsimd.memset(guess_pool[0:ROW, :], 0.0)
+        ones = held([P, P], F32, "ones")
+        quad_base = held([P, 1], F32, "quad_base")
+        nc.gpsimd.memset(ks_pool[:].bitcast(I32), 0)
+        nc.gpsimd.memset(ones[:], 1.0)
+        for g in range(P // QUAD):
+            nc.gpsimd.memset(quad_base[QUAD * g : QUAD * (g + 1), :], float(QUAD * g))
+        nc.vector.memset(thr_pool[0:ROW, :].bitcast(I32), 0)
+
+        count = held([P, P], F32, "count")
+        lane = held([P, QUAD], F32, "lane")
+        ident = held([P, P], F32, "ident")
+        nc.vector.tensor_tensor_scan(count[:], ones[:], ones[:], 0.0, ALU.mult, ALU.add)
+        nc.vector.memset(steep_pool[0:ROW, :].bitcast(I32), 0)
+        nc.vector.transpose(lane[:], count[:, 0:QUAD])
+        nc.vector.memset(guess_pool[0:ROW, :].bitcast(I32), 0)
+        nc.vector.tensor_scalar(ident[:], count[:], quad_base[:], lane[:, 0:1], ALU.subtract, ALU.is_equal)
 
         def row_numbers(queue, dst, src):
             with nc.allow_non_contiguous_dma(reason="one number a query row"):
                 queue.dma_start(dst[:], src[:, 0].rearrange("(u p) -> p u", p=P))
 
-        def key_scale_rows(queue, g):
-            queue.dma_start(
-                ks_pool[32 * g : 32 * g + 4, :].bitcast(I32), keys_scales[0, 4 * g : 4 * g + 4, :].bitcast(I32)
-            )
+        v_rows = vals.rearrange("(p t) n -> t p n", t=PACK)
+        nc.sync.dma_start(offs_t[:], offs)
+        nc.scalar.dma_start(thr_pool[ROW:P, :], thr[0:1, :])
+        nc.sync.dma_start(kw_pool[:].bitcast(I32), keys_words[0].bitcast(I32))
+        nc.scalar.dma_start(steep_pool[ROW:P, :], steep[0:1, :])
+        nc.sync.dma_start(q_raw[:], query.rearrange("(p j) q -> p j q", j=PACK))
+        nc.sync.dma_start(ks_pool[0 : 4, :].bitcast(I32), keys_scales[0, 0 : 4, :].bitcast(I32))
+        nc.sync.dma_start(ks_pool[32 : 36, :].bitcast(I32), keys_scales[0, 4 : 8, :].bitcast(I32))
+        nc.sync.dma_start(ks_pool[64 : 68, :].bitcast(I32), keys_scales[0, 8 : 12, :].bitcast(I32))
+        nc.sync.dma_start(ks_pool[96 : 100, :].bitcast(I32), keys_scales[0, 12 : 16, :].bitcast(I32))
+        nc.gpsimd.dma_start(guess_pool[ROW:P, :], guess[0:1, :])
+        nc.sync.dma_start(v_pool[0][:], v_rows[0])
+        nc.sync.dma_start(vsc_t[:], vsc[0].rearrange("(s r) -> s r", r=PACK))
+        row_numbers(nc.sync, lam_t, lam)
+        nc.sync.dma_start(v_pool[1][:], v_rows[1])
+        nc.sync.dma_start(os_t[:], slot_os[0].rearrange("(s r) -> s r", r=PACK))
+        row_numbers(nc.sync, eager_t, eager)
+        row_numbers(nc.sync, thresh_t, thresh)
+        nc.sync.dma_start(v_pool[2][:], v_rows[2])
+        nc.sync.dma_start(v_pool[3][:], v_rows[3])
 
-        def token_columns(row, b, name):
+        def token_columns(pool, on_scalar, b, name, tag=None):
+            row = held([P, I], F32, name + "_row", tag)
+            if on_scalar:
+                nc.scalar.activation(row[:], pool[:].indirect(offs_t[:]), ACT.Copy)
+            else:
+                nc.vector.tensor_copy(row[:], pool[:].indirect(offs_t[:]))
             turned = bank([P, 4, P], b, name + "_turned")
             for j in range(4):
                 nc.tensor.transpose(turned[:, j, :], row[:, j * P : (j + 1) * P], ident[:])
             return turned[:, :, ROW]
 
-        v_rows = vals.rearrange("(p t) n -> t p n", t=PACK)
-        out_rows = out_0.rearrange("(p t) q -> p t q", t=PACK)
-        v_codes = [held([P, P], U32, "v_codes%d" % t) for t in range(PACK)]
-        v_scales = [held([P, P], U8, "v_scales%d" % t) for t in range(PACK)]
-        o_bf = held([P, Q, PACK], BF16, "o_bf")
-        o_codes = held([P, Q], U32, "o_codes")
-        o_scales = held([P, Q], U8, "o_scales")
-        nc.sync.dma_start(offs_t[:], offs)
-        nc.scalar.dma_start(thr_pool[ROW:P, :], thr[0:1, :])
-        nc.sync.dma_start(kw_pool[:].bitcast(I32), keys_words[0].bitcast(I32))
-        nc.scalar.dma_start(steep_pool[ROW:P, :], steep[0:1, :])
-        key_scale_rows(nc.sync, 0)
-        key_scale_rows(nc.sync, 1)
-        key_scale_rows(nc.sync, 2)
-        key_scale_rows(nc.sync, 3)
-        nc.sync.dma_start(q_raw[:], query.rearrange("(p j) q -> p j q", j=PACK))
-        nc.sync.dma_start(v_pool[0][:], v_rows[0])
-        nc.sync.dma_start(guess_pool[ROW:P, :], guess[0:1, :])
-        nc.sync.dma_start(vsc_t[:], vsc[0].rearrange("(s r) -> s r", r=PACK))
-        nc.sync.dma_start(v_pool[1][:], v_rows[1])
-        row_numbers(nc.sync, lam_t, lam)
-        nc.sync.dma_start(v_pool[2][:], v_rows[2])
-        row_numbers(nc.sync, eager_t, eager)
-        row_numbers(nc.sync, thresh_t, thresh)
-        nc.sync.dma_start(os_t[:], slot_os[0].rearrange("(s r) -> s r", r=PACK))
-        nc.sync.dma_start(v_pool[3][:], v_rows[3])
+        picked = [None] * PACK
+        v_turned = [None] * PACK
+        v_mx = [None] * PACK
+
+        def gather_values(t, on_scalar, b, dealt, tag=None):
+            picked[t] = held([P, I], F32, "picked%d" % t, tag)
+            v_turned[t] = bank([P, PACK, P], b, "v_turned%d" % t)
+            if on_scalar:
+                nc.scalar.activation(picked[t][:], v_pool[t][:].indirect(offs_t[:]), ACT.Copy)
+                in_order = picked[t][:].rearrange("p (s r) -> p s r", r=PACK)
+            else:
+                in_order = picked[t][:].rearrange("p (r s) -> p s r" if dealt else "p (s r) -> p s r", r=PACK)
+                nc.vector.tensor_copy(in_order, v_pool[t][:].indirect(offs_t[:]))
+            for r in range(PACK):
+                nc.tensor.matmul(
+                    v_turned[t][:, r, :], in_order[:, :, r], ident[:], start=(r == 0), stop=False, is_transpose=True
+                )
+            return in_order
+
+        def take_means(t, in_order, tag=None):
+            sums = held([P, H], F32, "sums%d" % t, tag)
+            nc.vector.tensor_reduce(sums[:], in_order.rearrange("p (h u) r -> p h r u", h=H), AX.XY, ALU.add)
+            neg_mean = held([P, H, STRETCH // PACK], F32, "neg_mean%d" % t)
+            nc.vector.tensor_scalar(
+                neg_mean[:], sums[:].unsqueeze(2).to_broadcast([P, H, STRETCH // PACK]), -1.0 / STRETCH, None, ALU.mult
+            )
+            for r in range(PACK):
+                nc.tensor.matmul(
+                    v_turned[t][:, r, :], neg_mean[:].rearrange("p h u -> p (h u)"), ident[:],
+                    start=False, stop=(r == PACK - 1), is_transpose=True,
+                )
+
+        def scale_values(t, tag=None):
+            v_bf = held([P, P, PACK], BF16, "v_bf%d" % t, tag)
+            nc.vector.tensor_tensor(
+                v_bf[:], v_turned[t][:].rearrange("s r e -> s e r"),
+                vsc_t[:].unsqueeze(1).to_broadcast([P, P, PACK]), ALU.mult,
+            )
+            v_mx[t] = quantise(v_bf[:].rearrange("s e r -> s (e r)"), P, "v%d" % t)
+
+        warm = held([P, 1], F32, "warm")
+        nc.scalar.activation(warm[:], ones[:, 0:1], ACT.Sigmoid)
+
+        thr_col = token_columns(thr_pool, True, 2, "thr")
 
         kw = held([P, I], U16, "kw")
         nc.vector.tensor_copy(kw[:], kw_pool[:].indirect(offs_t[:]))
 
+        steep_col = token_columns(steep_pool, True, 3, "steep")
+
         ks = held([P, I], U8, "ks")
         nc.vector.tensor_copy(ks[:], ks_pool[:].indirect(offs_t[:]))
 
-        thr_row = held([P, I], F32, "thr_row")
-        nc.scalar.activation(thr_row[:], thr_pool[:].indirect(offs_t[:]), ACT.Copy)
-
-        thr_col = token_columns(thr_row, 4, "thr")
-
-        neg_thr = held([P, 4], F32, "neg_thr")
-        nc.vector.tensor_scalar(neg_thr[:], thr_col, -1.0, None, ALU.mult)
-
-        steep_row = held([P, I], F32, "steep_row")
-        nc.scalar.activation(steep_row[:], steep_pool[:].indirect(offs_t[:]), ACT.Copy)
-
-        steep_col = token_columns(steep_row, 5, "steep")
+        q_bf = held([P, Q, PACK], BF16, "q_bf")
+        nc.scalar.copy(q_bf[:], q_raw[:].rearrange("p j q -> p q j"))
 
         steep_c = held([P, 4], F32, "steep_c")
         shift_c = held([P, 4], F32, "shift_c")
-        nc.vector.tensor_tensor(shift_c[:], steep_col, neg_thr[:], ALU.mult)
         nc.vector.tensor_copy(steep_c[:], steep_col)
+        nc.vector.scalar_tensor_tensor(shift_c[:], thr_col, -1.0, steep_c[:], ALU.mult, ALU.mult)
 
-        q_bf = held([P, Q, PACK], BF16, "q_bf")
-        nc.vector.tensor_copy(q_bf[:], q_raw[:].rearrange("p j q -> p q j"))
-
-        q_codes = held([P, Q], U32, "q_codes")
-        q_scales = held([P, Q], U8, "q_scales")
-        nc.vector.quantize_mx(out=q_codes[:].bitcast(FP8X4), scales=q_scales[:], in_=q_bf[:].rearrange("p q j -> p (q j)"))
-
-        a_ps = [bank([P, Q], b, "a_ps%d" % b) for b in (0, 1, 2, 3)]
+        q_codes, q_scales = quantise(q_bf[:].rearrange("p q j -> p (q j)"), Q, "q")
+        a_ps = [bank([P, Q], b, "a_ps%d" % b) for b in (0, 1, 5, 7)]
         for j in range(4):
             nc.tensor.matmul_mx(
                 out=a_ps[j][:],
@@ -147,15 +213,9 @@ def tile_attend_answerodds_abstaining_centredvalues_pl_kernel(
                 stop=True,
             )
 
-        guess_row = held([P, I], F32, "guess_row")
-        nc.scalar.activation(guess_row[:], guess_pool[:].indirect(offs_t[:]), ACT.Copy)
+        guess_col = token_columns(guess_pool, True, 4, "guess")
 
-        guess_col = token_columns(guess_row, 4, "guess")
-
-        guess_c = held([P, 4], F32, "guess_c")
-        rest_c = held([P, 4], F32, "rest_c")
-        nc.vector.tensor_copy(guess_c[:], guess_col)
-        nc.vector.tensor_scalar(rest_c[:], guess_col, -1.0, 1.0, ALU.mult, ALU.add)
+        order0 = gather_values(0, False, 6, False)
 
         sg = [held([P, Q], F32, "sg%d" % j) for j in range(4)]
         for j in range(4):
@@ -163,29 +223,46 @@ def tile_attend_answerodds_abstaining_centredvalues_pl_kernel(
                 sg[j][:], a_ps[j][:], ACT.Sigmoid, bias=shift_c[:, j : j + 1], scale=steep_c[:, j : j + 1]
             )
 
+        os_all = bank([P, PACK, P], 0, "os_all")
+        for r in range(PACK):
+            nc.tensor.transpose(os_all[:, r, :], os_t[:, r : r + 1].to_broadcast([P, P]), ident[:])
+        w_mx = [None] * QT
+
+        take_means(0, order0)
+
+        guess_c = held([P, 4], F32, "guess_c")
+        rest_c = held([P, 4], F32, "rest_c")
+        nc.vector.tensor_copy(guess_c[:], guess_col)
+        nc.vector.tensor_scalar(rest_c[:], guess_col, -1.0, 1.0, ALU.mult, ALU.add)
         chance = [held([P, Q], F32, "chance%d" % j) for j in range(4)]
         for j in range(4):
             nc.vector.tensor_scalar(
                 chance[j][:], sg[j][:], rest_c[:, j : j + 1], guess_c[:, j : j + 1], ALU.mult, ALU.add
             )
-        chance_q = [bank([P, I], b, "chance_q%d" % b) for b in (4, 5)]
-        for j in range(4):
-            for u in range(QT):
-                nc.tensor.transpose(chance_q[u][:, j * P : (j + 1) * P], chance[j][:, u * P : (u + 1) * P], ident[:])
-
-        ln_q = [held([P, PACK, P], F32, "ln_q%d" % u) for u in range(QT)]
-        ln_sum = [held([P, 1], F32, "ln_sum%d" % u) for u in range(QT)]
+        chance_q = [bank([P, I], b, "chance_q%d" % b) for b in (3, 4)]
         for u in range(QT):
-            nc.scalar.activation(
-                ln_q[u][:], chance_q[u][:].rearrange("q (s r) -> q r s", r=PACK), ACT.Ln, accum_out=ln_sum[u][:]
-            )
+            for j in range(4):
+                nc.tensor.transpose(chance_q[u][:, j * P : (j + 1) * P], chance[j][:, u * P : (u + 1) * P], ident[:])
 
         neg_lam = held([P, QT], F32, "neg_lam")
         lam_mean = held([P, QT], F32, "lam_mean")
-        nc.vector.tensor_scalar(neg_lam[:], lam_t[:], -1.0, None, ALU.mult)
-        nc.vector.tensor_scalar(lam_mean[:], lam_t[:], 1.0 / I, None, ALU.mult)
+        nc.scalar.activation(neg_lam[:], lam_t[:], ACT.Copy, scale=-1.0)
+        nc.scalar.activation(lam_mean[:], lam_t[:], ACT.Copy, scale=1.0 / I)
 
-        neg_s = [held([P, PACK, P], F32, "neg_s%d" % u) for u in range(QT)]
+        order1 = gather_values(1, True, 7, False)
+
+        take_means(1, order1)
+
+        scale_values(0)
+
+        ln_q = [held([P, I], F32, "ln_q%d" % u) for u in range(QT)]
+        ln_sum = [held([P, 1], F32, "ln_sum%d" % u) for u in range(QT)]
+        for u in range(QT):
+            nc.scalar.activation(ln_q[u][:], chance_q[u][:], ACT.Ln, accum_out=ln_sum[u][:])
+
+        order2 = gather_values(2, False, 5, False)
+
+        neg_s = [held([P, I], F32, "neg_s%d" % u) for u in range(QT)]
         neg_m0 = [held([P, 1], F32, "neg_m0_%d" % u) for u in range(QT)]
         lag = held([P, QT], F32, "lag")
         for u in range(QT):
@@ -197,211 +274,95 @@ def tile_attend_answerodds_abstaining_centredvalues_pl_kernel(
                 lag[:, u : u + 1], ln_sum[u][:], lam_mean[:, u : u + 1], neg_m0[u][:], ALU.mult, ALU.add
             )
 
+        scale_values(1)
+
+        take_means(2, order2)
+
+        order3 = gather_values(3, True, 6, False)
+
+        take_means(3, order3)
+
         odds = held([P, QT], F32, "odds")
         for u in range(QT):
             nc.scalar.activation(
                 odds[:, u : u + 1], lag[:, u : u + 1], ACT.Exp, bias=thresh_t[:, u : u + 1], scale=eager_t[:, u : u + 1]
             )
 
-        odds1 = held([P, QT], F32, "odds1")
-        gate = held([P, QT], F32, "gate")
-        nc.vector.tensor_scalar(odds1[:], odds[:], 1.0, None, ALU.add)
-        nc.vector.reciprocal(gate[:], odds1[:])
+        p_t = [None] * QT
+        p_t[0] = held([P, I], F32, "p_t0")
+        p_sum0 = held([P, 1], F32, "p_sum0")
+        nc.scalar.activation(p_t[0][:], neg_s[0][:], ACT.Exp, bias=neg_m0[0][:], scale=-1.0, accum_out=p_sum0[:])
+        over0 = held([P, 1], F32, "over0")
+        nc.scalar.activation(over0[:], odds[:, 0 : 1], ACT.Identity, bias=p_sum0[:], scale=p_sum0[:])
 
-        p_t = [held([P, I], F32, "p_t%d" % u) for u in range(QT)]
-        p_sum = [held([P, 1], F32, "p_sum%d" % u) for u in range(QT)]
+        p_t[1] = held([P, I], F32, "p_t1")
+        p_sum1 = held([P, 1], F32, "p_sum1")
+        nc.scalar.activation(p_t[1][:], neg_s[1][:], ACT.Exp, bias=neg_m0[1][:], scale=-1.0, accum_out=p_sum1[:])
+        over1 = held([P, 1], F32, "over1")
+        nc.scalar.activation(over1[:], odds[:, 1 : 2], ACT.Identity, bias=p_sum1[:], scale=p_sum1[:])
+
+        scale_values(2)
+
+        share0 = held([P, 1], F32, "share0")
+        nc.vector.reciprocal(share0[:], over0[:])
+        w_q0 = held([P, P, PACK], BF16, "w_q0")
+        nc.vector.scalar_tensor_tensor(
+            w_q0[:], p_t[0][:].rearrange("q (s r) -> q s r", r=PACK), share0[:],
+            os_all[:].rearrange("q r s -> q s r"), ALU.mult, ALU.mult,
+        )
+        w_words0 = w_q0[:].rearrange("q s r -> q (s r)").bitcast(F32)
+        w_turned0 = bank([P, 2, P], 3, "w_turned0")
+        for h in range(2):
+            nc.tensor.transpose(w_turned0[:, h, :], w_words0[:, h : 2 * P : 2], ident[:])
+        w_bf0 = held([P, P, 2], F32, "w_bf0")
+        nc.scalar.copy(w_bf0[:], w_turned0[:].rearrange("s h q -> s q h"))
+
+        scale_values(3)
+
+        share1 = held([P, 1], F32, "share1")
+        nc.vector.reciprocal(share1[:], over1[:])
+        w_q1 = held([P, P, PACK], BF16, "w_q1")
+        nc.vector.scalar_tensor_tensor(
+            w_q1[:], p_t[1][:].rearrange("q (s r) -> q s r", r=PACK), share1[:],
+            os_all[:].rearrange("q r s -> q s r"), ALU.mult, ALU.mult,
+        )
+        w_words1 = w_q1[:].rearrange("q s r -> q (s r)").bitcast(F32)
+        w_turned1 = bank([P, 2, P], 4, "w_turned1")
+        for h in range(2):
+            nc.tensor.transpose(w_turned1[:, h, :], w_words1[:, h : 2 * P : 2], ident[:])
+        w_bf1 = held([P, P, 2], F32, "w_bf1")
+        nc.scalar.copy(w_bf1[:], w_turned1[:].rearrange("s h q -> s q h"))
+
+        w_mx[0] = quantise(w_bf0[:].rearrange("s q h -> s (q h)").bitcast(BF16), P, "w0")
+
+        w_mx[1] = quantise(w_bf1[:].rearrange("s q h -> s (q h)").bitcast(BF16), P, "w1")
+
+        out_rows = out_0.rearrange("(p t) q -> p t q", t=PACK)
+        o_ps = [bank([P, PACK, P], 1 + u, "o_ps%d" % u) for u in range(QT)]
         for u in range(QT):
-            nc.scalar.activation(
-                p_t[u][:], neg_s[u][:].rearrange("q r s -> q (r s)"), ACT.Exp,
-                bias=neg_m0[u][:], scale=-1.0, accum_out=p_sum[u][:],
+            for t in range(PACK):
+                nc.tensor.matmul_mx(
+                    out=o_ps[u][:, t, :],
+                    lhsT=v_mx[t][0][:].bitcast(FP8X4),
+                    lhsT_scale=v_mx[t][1][:],
+                    rhs=w_mx[u][0][:].bitcast(FP8X4),
+                    rhs_scale=w_mx[u][1][:],
+                    start=True,
+                    stop=True,
+                )
+        o_sb = [held([P, PACK, P], F32, "o_sb%d" % u) for u in range(QT)]
+        o_bf = [held([P, P, PACK], BF16, "o_bf%d" % u) for u in range(QT)]
+        o_codes = held([P, Q], U32, "o_codes")
+        o_scales = held([P, Q], U8, "o_scales")
+        for u in range(QT):
+            cols = slice(u * P, (u + 1) * P)
+            nc.vector.tensor_copy(o_bf[u][:], o_ps[u][:].rearrange("p t q -> p q t"))
+            nc.scalar.copy(o_sb[u][:], o_ps[u][:])
+            nc.sync.dma_start(out_rows[:, :, cols], o_sb[u][:])
+            nc.vector.quantize_mx(
+                out=o_codes[:, cols].bitcast(FP8X4), scales=o_scales[:, cols],
+                in_=o_bf[u][:].rearrange("p q t -> p (q t)"),
             )
-
-        inv_sum0 = held([P, 1], F32, "inv_sum0")
-        nc.vector.reciprocal(inv_sum0[:], p_sum[0][:])
-        w_t0 = held([P, I], F32, "w_t0")
-        nc.vector.tensor_scalar(w_t0[:], p_t[0][:], inv_sum0[:], gate[:, 0 : 1], ALU.mult, ALU.mult)
-        w_turned0 = bank([P, PACK, P], 0, "w_turned0")
-        for r in range(PACK):
-            nc.tensor.transpose(w_turned0[:, r, :], w_t0[:, r * P : (r + 1) * P], ident[:])
-
-        inv_sum1 = held([P, 1], F32, "inv_sum1")
-        nc.vector.reciprocal(inv_sum1[:], p_sum[1][:])
-        w_t1 = held([P, I], F32, "w_t1")
-        nc.vector.tensor_scalar(w_t1[:], p_t[1][:], inv_sum1[:], gate[:, 1 : 2], ALU.mult, ALU.mult)
-        w_turned1 = bank([P, PACK, P], 1, "w_turned1")
-        for r in range(PACK):
-            nc.tensor.transpose(w_turned1[:, r, :], w_t1[:, r * P : (r + 1) * P], ident[:])
-
-        w_bf0 = held([P, P, PACK], BF16, "w_bf0")
-        nc.vector.tensor_tensor(
-            w_bf0[:], w_turned0[:].rearrange("s r q -> s q r"), os_t[:].unsqueeze(1).to_broadcast([P, P, PACK]), ALU.mult
-        )
-
-        w_bf1 = held([P, P, PACK], BF16, "w_bf1")
-        nc.vector.tensor_tensor(
-            w_bf1[:], w_turned1[:].rearrange("s r q -> s q r"), os_t[:].unsqueeze(1).to_broadcast([P, P, PACK]), ALU.mult
-        )
-
-        w_codes0 = held([P, P], U32, "w_codes0")
-        w_scales0 = held([P, P], U8, "w_scales0")
-        nc.vector.quantize_mx(out=w_codes0[:].bitcast(FP8X4), scales=w_scales0[:], in_=w_bf0[:].rearrange("s q r -> s (q r)"))
-
-        w_codes1 = held([P, P], U32, "w_codes1")
-        w_scales1 = held([P, P], U8, "w_scales1")
-        nc.vector.quantize_mx(out=w_codes1[:].bitcast(FP8X4), scales=w_scales1[:], in_=w_bf1[:].rearrange("s q r -> s (q r)"))
-
-        picked0 = held([P, I], F32, "picked0")
-        nc.scalar.activation(picked0[:], v_pool[0][:].indirect(offs_t[:]), ACT.Copy)
-        v_turned0 = bank([P, PACK, P], 6, "v_turned0")
-        for r in range(PACK):
-            nc.tensor.matmul(
-                v_turned0[:, r, :], picked0[:, r:I:PACK], ident[:], start=(r == 0), stop=False, is_transpose=True
-            )
-        sums0 = held([P, H], F32, "sums0")
-        nc.vector.tensor_reduce(sums0[:], picked0[:].rearrange("p (h k) -> p h k", k=STRETCH), AX.X, ALU.add)
-        neg_mean0 = held([P, H, STRETCH // PACK], F32, "neg_mean0")
-        nc.vector.tensor_scalar(neg_mean0[:], sums0[:].unsqueeze(2).to_broadcast([P, H, STRETCH // PACK]), -1.0 / STRETCH, None, ALU.mult)
-        for r in range(PACK):
-            nc.tensor.matmul(
-                v_turned0[:, r, :], neg_mean0[:].rearrange("p h u -> p (h u)"), ident[:], start=False, stop=(r == PACK - 1), is_transpose=True
-            )
-        v_bf0 = held([P, P, PACK], BF16, "v_bf0")
-        nc.vector.tensor_tensor(
-            v_bf0[:], v_turned0[:].rearrange("s r e -> s e r"), vsc_t[:].unsqueeze(1).to_broadcast([P, P, PACK]), ALU.mult
-        )
-        nc.vector.quantize_mx(out=v_codes[0][:].bitcast(FP8X4), scales=v_scales[0][:], in_=v_bf0[:].rearrange("s e r -> s (e r)"))
-
-        picked1 = held([P, I], F32, "picked1")
-        nc.vector.tensor_copy(picked1[:].rearrange("p (r s) -> p s r", r=PACK), v_pool[1][:].indirect(offs_t[:]))
-        v_turned1 = bank([P, PACK, P], 7, "v_turned1")
-        for r in range(PACK):
-            nc.tensor.matmul(
-                v_turned1[:, r, :], picked1[:, r * P : (r + 1) * P], ident[:], start=(r == 0), stop=False, is_transpose=True
-            )
-        sums1 = held([P, H], F32, "sums1")
-        nc.vector.tensor_reduce(sums1[:], picked1[:].rearrange("p (r h u) -> p h r u", r=PACK, h=H), AX.XY, ALU.add)
-        neg_mean1 = held([P, H, STRETCH // PACK], F32, "neg_mean1")
-        nc.vector.tensor_scalar(neg_mean1[:], sums1[:].unsqueeze(2).to_broadcast([P, H, STRETCH // PACK]), -1.0 / STRETCH, None, ALU.mult)
-        for r in range(PACK):
-            nc.tensor.matmul(
-                v_turned1[:, r, :], neg_mean1[:].rearrange("p h u -> p (h u)"), ident[:], start=False, stop=(r == PACK - 1), is_transpose=True
-            )
-        v_bf1 = held([P, P, PACK], BF16, "v_bf1")
-        nc.vector.tensor_tensor(
-            v_bf1[:], v_turned1[:].rearrange("s r e -> s e r"), vsc_t[:].unsqueeze(1).to_broadcast([P, P, PACK]), ALU.mult
-        )
-        nc.vector.quantize_mx(out=v_codes[1][:].bitcast(FP8X4), scales=v_scales[1][:], in_=v_bf1[:].rearrange("s e r -> s (e r)"))
-
-        picked2 = held([P, I], F32, "picked2")
-        nc.scalar.activation(picked2[:], v_pool[2][:].indirect(offs_t[:]), ACT.Copy)
-        v_turned2 = bank([P, PACK, P], 6, "v_turned2")
-        for r in range(PACK):
-            nc.tensor.matmul(
-                v_turned2[:, r, :], picked2[:, r:I:PACK], ident[:], start=(r == 0), stop=False, is_transpose=True
-            )
-        sums2 = held([P, H], F32, "sums2")
-        nc.vector.tensor_reduce(sums2[:], picked2[:].rearrange("p (h k) -> p h k", k=STRETCH), AX.X, ALU.add)
-        neg_mean2 = held([P, H, STRETCH // PACK], F32, "neg_mean2")
-        nc.vector.tensor_scalar(neg_mean2[:], sums2[:].unsqueeze(2).to_broadcast([P, H, STRETCH // PACK]), -1.0 / STRETCH, None, ALU.mult)
-        for r in range(PACK):
-            nc.tensor.matmul(
-                v_turned2[:, r, :], neg_mean2[:].rearrange("p h u -> p (h u)"), ident[:], start=False, stop=(r == PACK - 1), is_transpose=True
-            )
-        v_bf2 = held([P, P, PACK], BF16, "v_bf2")
-        nc.vector.tensor_tensor(
-            v_bf2[:], v_turned2[:].rearrange("s r e -> s e r"), vsc_t[:].unsqueeze(1).to_broadcast([P, P, PACK]), ALU.mult
-        )
-        nc.vector.quantize_mx(out=v_codes[2][:].bitcast(FP8X4), scales=v_scales[2][:], in_=v_bf2[:].rearrange("s e r -> s (e r)"))
-
-        picked3 = held([P, I], F32, "picked3")
-        nc.scalar.activation(picked3[:], v_pool[3][:].indirect(offs_t[:]), ACT.Copy)
-        v_turned3 = bank([P, PACK, P], 7, "v_turned3")
-        for r in range(PACK):
-            nc.tensor.matmul(
-                v_turned3[:, r, :], picked3[:, r:I:PACK], ident[:], start=(r == 0), stop=False, is_transpose=True
-            )
-        sums3 = held([P, H], F32, "sums3")
-        nc.vector.tensor_reduce(sums3[:], picked3[:].rearrange("p (h k) -> p h k", k=STRETCH), AX.X, ALU.add)
-        neg_mean3 = held([P, H, STRETCH // PACK], F32, "neg_mean3")
-        nc.vector.tensor_scalar(neg_mean3[:], sums3[:].unsqueeze(2).to_broadcast([P, H, STRETCH // PACK]), -1.0 / STRETCH, None, ALU.mult)
-        for r in range(PACK):
-            nc.tensor.matmul(
-                v_turned3[:, r, :], neg_mean3[:].rearrange("p h u -> p (h u)"), ident[:], start=False, stop=(r == PACK - 1), is_transpose=True
-            )
-        v_bf3 = held([P, P, PACK], BF16, "v_bf3")
-        nc.vector.tensor_tensor(
-            v_bf3[:], v_turned3[:].rearrange("s r e -> s e r"), vsc_t[:].unsqueeze(1).to_broadcast([P, P, PACK]), ALU.mult
-        )
-        nc.vector.quantize_mx(out=v_codes[3][:].bitcast(FP8X4), scales=v_scales[3][:], in_=v_bf3[:].rearrange("s e r -> s (e r)"))
-
-        o_sb0 = held([P, PACK, P], F32, "o_sb0")
-        o_ps = bank([P, 2, P], 2, "o_ps0_0")
-        for k in range(2):
-            nc.tensor.matmul_mx(
-                out=o_ps[:, k, :],
-                lhsT=v_codes[0 + k][:].bitcast(FP8X4),
-                lhsT_scale=v_scales[0 + k][:],
-                rhs=w_codes0[:].bitcast(FP8X4),
-                rhs_scale=w_scales0[:],
-                start=True,
-                stop=True,
-            )
-        nc.scalar.copy(o_sb0[:, 0 : 2, :], o_ps[:])
-        o_ps = bank([P, 2, P], 3, "o_ps0_1")
-        for k in range(2):
-            nc.tensor.matmul_mx(
-                out=o_ps[:, k, :],
-                lhsT=v_codes[2 + k][:].bitcast(FP8X4),
-                lhsT_scale=v_scales[2 + k][:],
-                rhs=w_codes0[:].bitcast(FP8X4),
-                rhs_scale=w_scales0[:],
-                start=True,
-                stop=True,
-            )
-        nc.scalar.copy(o_sb0[:, 2 : 4, :], o_ps[:])
-        nc.sync.dma_start(out_rows[:, :, 0 : 128], o_sb0[:])
-
-        o_sb1 = held([P, PACK, P], F32, "o_sb1")
-        o_ps = bank([P, 2, P], 4, "o_ps1_0")
-        for k in range(2):
-            nc.tensor.matmul_mx(
-                out=o_ps[:, k, :],
-                lhsT=v_codes[0 + k][:].bitcast(FP8X4),
-                lhsT_scale=v_scales[0 + k][:],
-                rhs=w_codes1[:].bitcast(FP8X4),
-                rhs_scale=w_scales1[:],
-                start=True,
-                stop=True,
-            )
-        nc.vector.tensor_copy(o_sb1[:, 0 : 2, :], o_ps[:])
-        o_ps = bank([P, 2, P], 5, "o_ps1_1")
-        for k in range(2):
-            nc.tensor.matmul_mx(
-                out=o_ps[:, k, :],
-                lhsT=v_codes[2 + k][:].bitcast(FP8X4),
-                lhsT_scale=v_scales[2 + k][:],
-                rhs=w_codes1[:].bitcast(FP8X4),
-                rhs_scale=w_scales1[:],
-                start=True,
-                stop=True,
-            )
-        nc.scalar.copy(o_sb1[:, 2 : 4, :], o_ps[:])
-        nc.sync.dma_start(out_rows[:, :, 128 : 256], o_sb1[:])
-
-        nc.vector.tensor_copy(o_bf[:, 0 : 128, :], o_sb0[:].rearrange("p t q -> p q t"))
-
-        nc.vector.tensor_copy(o_bf[:, 128 : 256, :], o_sb1[:].rearrange("p t q -> p q t"))
-
-        nc.vector.quantize_mx(
-            out=o_codes[:, 0 : 128].bitcast(FP8X4), scales=o_scales[:, 0 : 128],
-            in_=o_bf[:, 0 : 128, :].rearrange("p q t -> p (q t)"),
-        )
-
-        nc.vector.quantize_mx(
-            out=o_codes[:, 128 : 256].bitcast(FP8X4), scales=o_scales[:, 128 : 256],
-            in_=o_bf[:, 128 : 256, :].rearrange("p q t -> p (q t)"),
-        )
-
         nc.sync.dma_start(out_1[0].rearrange("p q r -> p (q r)").bitcast(I32), o_codes[:].bitcast(I32))
         for g in range(4):
             queue = nc.scalar if g % 2 == 0 else nc.sync

@@ -36,15 +36,25 @@ PLACES = {
     "neg_s0": 16384,
     "neg_s1": 18432,
     "v0_codes": 20480,
+    "neg_lam": 20992,
+    "lam_mean": 21120,
     "v_pool0": 24576,
-    "neg_lam": 24576,
-    "lam_mean": 24704,
-    "sums1": 32768,
-    "v_bf0": 32768,
+    "guess_c": 24576,
+    "rest_c": 24704,
+    "ks_pool": 32768,
+    "steep_c": 32768,
+    "q_codes": 32896,
+    "sums1": 34816,
+    "v_bf0": 34816,
     "v_bf1": 2048,
-    "sums3": 33792,
-    "v_bf2": 33792,
-    "v_bf3": 8192
+    "sums3": 35840,
+    "v_bf2": 35840,
+    "v_bf3": 8192,
+    "over0": 36864,
+    "v2_codes": 36864,
+    "sums2": 0,
+    "shift_c": 37376,
+    "picked1": 37376
 }
 
 
@@ -110,30 +120,30 @@ def tile_attend_answerodds_abstaining_centredvalues_pl_kernel(
         v_rows = vals.rearrange("(p t) n -> t p n", t=PACK)
         nc.sync.dma_start(offs_t[:], offs)
         nc.scalar.dma_start(thr_pool[ROW:P, :], thr[0:1, :])
-        nc.sync.dma_start(kw_pool[:].bitcast(I32), keys_words[0].bitcast(I32))
         nc.scalar.dma_start(steep_pool[ROW:P, :], steep[0:1, :])
+        nc.sync.dma_start(guess_pool[ROW:P, :], guess[0:1, :])
+        nc.sync.dma_start(kw_pool[:].bitcast(I32), keys_words[0].bitcast(I32))
         nc.sync.dma_start(q_raw[:], query.rearrange("(p j) q -> p j q", j=PACK))
         nc.sync.dma_start(ks_pool[0 : 4, :].bitcast(I32), keys_scales[0, 0 : 4, :].bitcast(I32))
         nc.sync.dma_start(ks_pool[32 : 36, :].bitcast(I32), keys_scales[0, 4 : 8, :].bitcast(I32))
         nc.sync.dma_start(ks_pool[64 : 68, :].bitcast(I32), keys_scales[0, 8 : 12, :].bitcast(I32))
         nc.sync.dma_start(ks_pool[96 : 100, :].bitcast(I32), keys_scales[0, 12 : 16, :].bitcast(I32))
-        nc.gpsimd.dma_start(guess_pool[ROW:P, :], guess[0:1, :])
         nc.sync.dma_start(v_pool[0][:], v_rows[0])
         nc.sync.dma_start(vsc_t[:], vsc[0].rearrange("(s r) -> s r", r=PACK))
-        row_numbers(nc.sync, lam_t, lam)
         nc.sync.dma_start(v_pool[1][:], v_rows[1])
+        nc.sync.dma_start(v_pool[2][:], v_rows[2])
+        row_numbers(nc.sync, lam_t, lam)
+        nc.sync.dma_start(v_pool[3][:], v_rows[3])
         nc.sync.dma_start(os_t[:], slot_os[0].rearrange("(s r) -> s r", r=PACK))
         row_numbers(nc.sync, eager_t, eager)
         row_numbers(nc.sync, thresh_t, thresh)
-        nc.sync.dma_start(v_pool[2][:], v_rows[2])
-        nc.sync.dma_start(v_pool[3][:], v_rows[3])
 
-        def token_columns(pool, on_scalar, b, name, tag=None):
-            row = held([P, I], F32, name + "_row", tag)
-            if on_scalar:
-                nc.scalar.activation(row[:], pool[:].indirect(offs_t[:]), ACT.Copy)
-            else:
-                nc.vector.tensor_copy(row[:], pool[:].indirect(offs_t[:]))
+        def token_row(pool, name):
+            row = held([P, I], F32, name + "_row")
+            nc.scalar.activation(row[:], pool[:].indirect(offs_t[:]), ACT.Copy)
+            return row
+
+        def token_columns(row, b, name):
             turned = bank([P, 4, P], b, name + "_turned")
             for j in range(4):
                 nc.tensor.transpose(turned[:, j, :], row[:, j * P : (j + 1) * P], ident[:])
@@ -156,11 +166,13 @@ def tile_attend_answerodds_abstaining_centredvalues_pl_kernel(
                 nc.tensor.matmul(
                     v_turned[t][:, r, :], in_order[:, :, r], ident[:], start=(r == 0), stop=False, is_transpose=True
                 )
-            return in_order
+            if dealt:
+                return picked[t][:].rearrange("p (r h u) -> p h r u", r=PACK, h=H)
+            return picked[t][:].rearrange("p (h u r) -> p h u r", r=PACK, h=H)
 
         def take_means(t, in_order, tag=None):
             sums = held([P, H], F32, "sums%d" % t, tag)
-            nc.vector.tensor_reduce(sums[:], in_order.rearrange("p (h u) r -> p h r u", h=H), AX.XY, ALU.add)
+            nc.vector.tensor_reduce(sums[:], in_order, AX.XY, ALU.add)
             neg_mean = held([P, H, STRETCH // PACK], F32, "neg_mean%d" % t)
             nc.vector.tensor_scalar(
                 neg_mean[:], sums[:].unsqueeze(2).to_broadcast([P, H, STRETCH // PACK]), -1.0 / STRETCH, None, ALU.mult
@@ -177,23 +189,25 @@ def tile_attend_answerodds_abstaining_centredvalues_pl_kernel(
                 v_bf[:], v_turned[t][:].rearrange("s r e -> s e r"),
                 vsc_t[:].unsqueeze(1).to_broadcast([P, P, PACK]), ALU.mult,
             )
-            v_mx[t] = quantise(v_bf[:].rearrange("s e r -> s (e r)"), P, "v%d" % t)
+            return v_bf[:].rearrange("s e r -> s (e r)")
 
         warm = held([P, 1], F32, "warm")
         nc.scalar.activation(warm[:], ones[:, 0:1], ACT.Sigmoid)
 
-        thr_col = token_columns(thr_pool, True, 2, "thr")
+        thr_col = token_columns(token_row(thr_pool, "thr"), 2, "thr")
 
         kw = held([P, I], U16, "kw")
         nc.vector.tensor_copy(kw[:], kw_pool[:].indirect(offs_t[:]))
 
-        steep_col = token_columns(steep_pool, True, 3, "steep")
+        steep_col = token_columns(token_row(steep_pool, "steep"), 3, "steep")
 
         ks = held([P, I], U8, "ks")
         nc.vector.tensor_copy(ks[:], ks_pool[:].indirect(offs_t[:]))
 
         q_bf = held([P, Q, PACK], BF16, "q_bf")
-        nc.scalar.copy(q_bf[:], q_raw[:].rearrange("p j q -> p q j"))
+        nc.scalar.copy(
+            q_bf[:].rearrange("p (c i) j -> p c j i", i=PACK), q_raw[:].rearrange("p j (c i) -> p c j i", i=PACK)
+        )
 
         steep_c = held([P, 4], F32, "steep_c")
         shift_c = held([P, 4], F32, "shift_c")
@@ -213,9 +227,9 @@ def tile_attend_answerodds_abstaining_centredvalues_pl_kernel(
                 stop=True,
             )
 
-        guess_col = token_columns(guess_pool, True, 4, "guess")
+        guess_row = token_row(guess_pool, "guess")
 
-        order0 = gather_values(0, False, 6, False)
+        order0 = gather_values(0, False, 6, True)
 
         sg = [held([P, Q], F32, "sg%d" % j) for j in range(4)]
         for j in range(4):
@@ -223,10 +237,7 @@ def tile_attend_answerodds_abstaining_centredvalues_pl_kernel(
                 sg[j][:], a_ps[j][:], ACT.Sigmoid, bias=shift_c[:, j : j + 1], scale=steep_c[:, j : j + 1]
             )
 
-        os_all = bank([P, PACK, P], 0, "os_all")
-        for r in range(PACK):
-            nc.tensor.transpose(os_all[:, r, :], os_t[:, r : r + 1].to_broadcast([P, P]), ident[:])
-        w_mx = [None] * QT
+        guess_col = token_columns(guess_row, 0, "guess")
 
         take_means(0, order0)
 
@@ -244,23 +255,30 @@ def tile_attend_answerodds_abstaining_centredvalues_pl_kernel(
             for j in range(4):
                 nc.tensor.transpose(chance_q[u][:, j * P : (j + 1) * P], chance[j][:, u * P : (u + 1) * P], ident[:])
 
-        neg_lam = held([P, QT], F32, "neg_lam")
-        lam_mean = held([P, QT], F32, "lam_mean")
-        nc.scalar.activation(neg_lam[:], lam_t[:], ACT.Copy, scale=-1.0)
-        nc.scalar.activation(lam_mean[:], lam_t[:], ACT.Copy, scale=1.0 / I)
-
         order1 = gather_values(1, True, 7, False)
 
         take_means(1, order1)
 
-        scale_values(0)
+        v_bf0 = scale_values(0)
+
+        os_all = bank([P, PACK, P], 6, "os_all")
+        for r in range(PACK):
+            nc.tensor.transpose(os_all[:, r, :], os_t[:, r : r + 1].to_broadcast([P, P]), ident[:])
+        w_mx = [None] * QT
 
         ln_q = [held([P, I], F32, "ln_q%d" % u) for u in range(QT)]
         ln_sum = [held([P, 1], F32, "ln_sum%d" % u) for u in range(QT)]
         for u in range(QT):
             nc.scalar.activation(ln_q[u][:], chance_q[u][:], ACT.Ln, accum_out=ln_sum[u][:])
 
-        order2 = gather_values(2, False, 5, False)
+        order2 = gather_values(2, False, 5, True)
+
+        neg_lam = held([P, QT], F32, "neg_lam")
+        lam_mean = held([P, QT], F32, "lam_mean")
+        nc.vector.tensor_scalar(neg_lam[:], lam_t[:], -1.0, None, ALU.mult)
+        nc.vector.tensor_scalar(lam_mean[:], lam_t[:], 1.0 / I, None, ALU.mult)
+
+        v_mx[0] = quantise(v_bf0, P, "v0")
 
         neg_s = [held([P, I], F32, "neg_s%d" % u) for u in range(QT)]
         neg_m0 = [held([P, 1], F32, "neg_m0_%d" % u) for u in range(QT)]
@@ -274,11 +292,13 @@ def tile_attend_answerodds_abstaining_centredvalues_pl_kernel(
                 lag[:, u : u + 1], ln_sum[u][:], lam_mean[:, u : u + 1], neg_m0[u][:], ALU.mult, ALU.add
             )
 
-        scale_values(1)
-
         take_means(2, order2)
 
-        order3 = gather_values(3, True, 6, False)
+        v_bf1 = scale_values(1)
+
+        v_mx[1] = quantise(v_bf1, P, "v1")
+
+        order3 = gather_values(3, True, 1, False)
 
         take_means(3, order3)
 
@@ -301,10 +321,14 @@ def tile_attend_answerodds_abstaining_centredvalues_pl_kernel(
         over1 = held([P, 1], F32, "over1")
         nc.scalar.activation(over1[:], odds[:, 1 : 2], ACT.Identity, bias=p_sum1[:], scale=p_sum1[:])
 
-        scale_values(2)
+        v_bf2 = scale_values(2)
 
         share0 = held([P, 1], F32, "share0")
         nc.vector.reciprocal(share0[:], over0[:])
+
+        share1 = held([P, 1], F32, "share1")
+        nc.vector.reciprocal(share1[:], over1[:])
+
         w_q0 = held([P, P, PACK], BF16, "w_q0")
         nc.vector.scalar_tensor_tensor(
             w_q0[:], p_t[0][:].rearrange("q (s r) -> q s r", r=PACK), share0[:],
@@ -317,10 +341,6 @@ def tile_attend_answerodds_abstaining_centredvalues_pl_kernel(
         w_bf0 = held([P, P, 2], F32, "w_bf0")
         nc.scalar.copy(w_bf0[:], w_turned0[:].rearrange("s h q -> s q h"))
 
-        scale_values(3)
-
-        share1 = held([P, 1], F32, "share1")
-        nc.vector.reciprocal(share1[:], over1[:])
         w_q1 = held([P, P, PACK], BF16, "w_q1")
         nc.vector.scalar_tensor_tensor(
             w_q1[:], p_t[1][:].rearrange("q (s r) -> q s r", r=PACK), share1[:],
@@ -333,12 +353,18 @@ def tile_attend_answerodds_abstaining_centredvalues_pl_kernel(
         w_bf1 = held([P, P, 2], F32, "w_bf1")
         nc.scalar.copy(w_bf1[:], w_turned1[:].rearrange("s h q -> s q h"))
 
+        v_mx[2] = quantise(v_bf2, P, "v2")
+
+        v_bf3 = scale_values(3)
+
         w_mx[0] = quantise(w_bf0[:].rearrange("s q h -> s (q h)").bitcast(BF16), P, "w0")
+
+        v_mx[3] = quantise(v_bf3, P, "v3")
 
         w_mx[1] = quantise(w_bf1[:].rearrange("s q h -> s (q h)").bitcast(BF16), P, "w1")
 
         out_rows = out_0.rearrange("(p t) q -> p t q", t=PACK)
-        o_ps = [bank([P, PACK, P], 1 + u, "o_ps%d" % u) for u in range(QT)]
+        o_ps = [bank([P, PACK, P], 2 * u, "o_ps%d" % u) for u in range(QT)]
         for u in range(QT):
             for t in range(PACK):
                 nc.tensor.matmul_mx(
@@ -358,12 +384,12 @@ def tile_attend_answerodds_abstaining_centredvalues_pl_kernel(
             cols = slice(u * P, (u + 1) * P)
             nc.vector.tensor_copy(o_bf[u][:], o_ps[u][:].rearrange("p t q -> p q t"))
             nc.scalar.copy(o_sb[u][:], o_ps[u][:])
-            nc.sync.dma_start(out_rows[:, :, cols], o_sb[u][:])
+            (nc.sync, nc.scalar)[u].dma_start(out_rows[:, :, cols], o_sb[u][:])
             nc.vector.quantize_mx(
                 out=o_codes[:, cols].bitcast(FP8X4), scales=o_scales[:, cols],
                 in_=o_bf[u][:].rearrange("p q t -> p (q t)"),
             )
         nc.sync.dma_start(out_1[0].rearrange("p q r -> p (q r)").bitcast(I32), o_codes[:].bitcast(I32))
         for g in range(4):
-            queue = nc.scalar if g % 2 == 0 else nc.sync
+            queue = nc.scalar if g == 3 else nc.sync
             queue.dma_start(out_2[0, 4 * g : 4 * g + 4, :].bitcast(I32), o_scales[32 * g : 32 * g + 4, :].bitcast(I32))

@@ -22,40 +22,30 @@ PACK = 4
 QUAD = 32
 STRETCH = 16
 H = I // STRETCH
+SLOT_TILES = I // P
 QT = Q // P
 ROW = P - 1
-PLACES = {
-    "v_pool1": 0,
-    "ln_q0": 0,
-    "ln_q1": 2048,
-    "v_pool3": 8192,
-    "p_t0": 8192,
-    "p_t1": 10240,
-    "odds": 12288,
-    "v_pool2": 16384,
-    "neg_s0": 16384,
-    "neg_s1": 18432,
-    "v0_codes": 20480,
-    "neg_lam": 20992,
-    "lam_mean": 21120,
-    "v_pool0": 24576,
-    "guess_c": 24576,
-    "rest_c": 24704,
-    "ks_pool": 32768,
-    "steep_c": 32768,
-    "q_codes": 32896,
-    "sums1": 34816,
-    "v_bf0": 34816,
-    "v_bf1": 2048,
-    "sums3": 35840,
-    "v_bf2": 35840,
-    "v_bf3": 8192,
-    "over0": 36864,
-    "v2_codes": 36864,
-    "sums2": 0,
-    "shift_c": 37376,
-    "picked1": 37376
-}
+
+TAKEOVERS = (
+    ("ks_pool", 2048, (("steep_c", 0), ("q_codes", 128))),
+    ("v_pool0", 8192, (("guess_c", 0), ("rest_c", 128))),
+    ("sg3", 1024, (("neg_lam", 0), ("lam_mean", 128))),
+    ("shift_c", 2048, (("picked1", 0),)),
+    ("v_pool1", 8192, (("chance3", 0),)),
+    ("v_pool2", 8192, (("neg_s0", 0), ("neg_s1", 2048), ("neg_mean1", 4096), ("v0_codes", 4608))),
+    ("v_pool3", 8192, (("p0", 0), ("p1", 2048), ("odds", 4096), ("v_bf3", 0))),
+)
+
+
+def shared_offsets():
+    offsets = {}
+    start = 0
+    for first, room, newcomers in TAKEOVERS:
+        offsets[first] = start
+        for name, at in newcomers:
+            offsets[name] = start + at
+        start = start + room
+    return offsets
 
 
 def tile_attend_answerodds_abstaining_centredvalues_pl_kernel(
@@ -63,14 +53,15 @@ def tile_attend_answerodds_abstaining_centredvalues_pl_kernel(
     out_0, out_1, out_2,
 ):
     nc = tc.nc
+    offsets = shared_offsets()
     with ExitStack() as ctx:
         sb = ctx.enter_context(tc.tile_pool(name="sb", bufs=1))
         shared = ctx.enter_context(tc.tile_pool(name="shared", bufs=1))
         ps = ctx.enter_context(tc.psum_pool(name="ps", bufs=1))
 
-        def held(shape, dtype, name, tag=None):
-            if name in PLACES:
-                return shared.tile(shape, dtype, name=name, align_bytes=64, offset=PLACES[name])
+        def held(shape, dtype, name):
+            if name in offsets:
+                return shared.tile(shape, dtype, name=name, align_bytes=64, offset=offsets[name])
             return sb.tile(shape, dtype, name=name, align_bytes=64)
 
         def bank(shape, b, name):
@@ -98,24 +89,26 @@ def tile_attend_answerodds_abstaining_centredvalues_pl_kernel(
 
         ones = held([P, P], F32, "ones")
         quad_base = held([P, 1], F32, "quad_base")
+        count = held([P, P], F32, "count")
+        lane = held([P, QUAD], F32, "lane")
+        ident = held([P, P], F32, "ident")
         nc.gpsimd.memset(ks_pool[:].bitcast(I32), 0)
         nc.gpsimd.memset(ones[:], 1.0)
         for g in range(P // QUAD):
             nc.gpsimd.memset(quad_base[QUAD * g : QUAD * (g + 1), :], float(QUAD * g))
         nc.vector.memset(thr_pool[0:ROW, :].bitcast(I32), 0)
-
-        count = held([P, P], F32, "count")
-        lane = held([P, QUAD], F32, "lane")
-        ident = held([P, P], F32, "ident")
         nc.vector.tensor_tensor_scan(count[:], ones[:], ones[:], 0.0, ALU.mult, ALU.add)
         nc.vector.memset(steep_pool[0:ROW, :].bitcast(I32), 0)
         nc.vector.transpose(lane[:], count[:, 0:QUAD])
         nc.vector.memset(guess_pool[0:ROW, :].bitcast(I32), 0)
         nc.vector.tensor_scalar(ident[:], count[:], quad_base[:], lane[:, 0:1], ALU.subtract, ALU.is_equal)
 
-        def row_numbers(queue, dst, src):
+        def load_by_query(dst, src):
             with nc.allow_non_contiguous_dma(reason="one number a query row"):
-                queue.dma_start(dst[:], src[:, 0].rearrange("(u p) -> p u", p=P))
+                nc.sync.dma_start(dst[:], src[:, 0].rearrange("(u p) -> p u", p=P))
+
+        def load_by_slot(dst, src):
+            nc.sync.dma_start(dst[:], src[0].rearrange("(s r) -> s r", r=PACK))
 
         v_rows = vals.rearrange("(p t) n -> t p n", t=PACK)
         nc.sync.dma_start(offs_t[:], offs)
@@ -123,20 +116,20 @@ def tile_attend_answerodds_abstaining_centredvalues_pl_kernel(
         nc.scalar.dma_start(steep_pool[ROW:P, :], steep[0:1, :])
         nc.sync.dma_start(guess_pool[ROW:P, :], guess[0:1, :])
         nc.sync.dma_start(kw_pool[:].bitcast(I32), keys_words[0].bitcast(I32))
-        nc.sync.dma_start(q_raw[:], query.rearrange("(p j) q -> p j q", j=PACK))
-        nc.sync.dma_start(ks_pool[0 : 4, :].bitcast(I32), keys_scales[0, 0 : 4, :].bitcast(I32))
-        nc.sync.dma_start(ks_pool[32 : 36, :].bitcast(I32), keys_scales[0, 4 : 8, :].bitcast(I32))
-        nc.sync.dma_start(ks_pool[64 : 68, :].bitcast(I32), keys_scales[0, 8 : 12, :].bitcast(I32))
-        nc.sync.dma_start(ks_pool[96 : 100, :].bitcast(I32), keys_scales[0, 12 : 16, :].bitcast(I32))
+        nc.sync.dma_start(q_raw[:], query.rearrange("(p r) q -> p r q", r=PACK))
+        for g in range(P // QUAD):
+            nc.sync.dma_start(
+                ks_pool[QUAD * g : QUAD * g + 4, :].bitcast(I32), keys_scales[0, 4 * g : 4 * g + 4, :].bitcast(I32)
+            )
         nc.sync.dma_start(v_pool[0][:], v_rows[0])
-        nc.sync.dma_start(vsc_t[:], vsc[0].rearrange("(s r) -> s r", r=PACK))
+        load_by_slot(vsc_t, vsc)
         nc.sync.dma_start(v_pool[1][:], v_rows[1])
+        load_by_query(lam_t, lam)
         nc.sync.dma_start(v_pool[2][:], v_rows[2])
-        row_numbers(nc.sync, lam_t, lam)
         nc.sync.dma_start(v_pool[3][:], v_rows[3])
-        nc.sync.dma_start(os_t[:], slot_os[0].rearrange("(s r) -> s r", r=PACK))
-        row_numbers(nc.sync, eager_t, eager)
-        row_numbers(nc.sync, thresh_t, thresh)
+        load_by_slot(os_t, slot_os)
+        load_by_query(eager_t, eager)
+        load_by_query(thresh_t, thresh)
 
         def token_row(pool, name):
             row = held([P, I], F32, name + "_row")
@@ -144,35 +137,39 @@ def tile_attend_answerodds_abstaining_centredvalues_pl_kernel(
             return row
 
         def token_columns(row, b, name):
-            turned = bank([P, 4, P], b, name + "_turned")
-            for j in range(4):
+            turned = bank([P, SLOT_TILES, P], b, name + "_turned")
+            for j in range(SLOT_TILES):
                 nc.tensor.transpose(turned[:, j, :], row[:, j * P : (j + 1) * P], ident[:])
             return turned[:, :, ROW]
 
-        picked = [None] * PACK
         v_turned = [None] * PACK
-        v_mx = [None] * PACK
 
-        def gather_values(t, on_scalar, b, dealt, tag=None):
-            picked[t] = held([P, I], F32, "picked%d" % t, tag)
+        def turn_values(t, by_slot, b):
             v_turned[t] = bank([P, PACK, P], b, "v_turned%d" % t)
-            if on_scalar:
-                nc.scalar.activation(picked[t][:], v_pool[t][:].indirect(offs_t[:]), ACT.Copy)
-                in_order = picked[t][:].rearrange("p (s r) -> p s r", r=PACK)
-            else:
-                in_order = picked[t][:].rearrange("p (r s) -> p s r" if dealt else "p (s r) -> p s r", r=PACK)
-                nc.vector.tensor_copy(in_order, v_pool[t][:].indirect(offs_t[:]))
             for r in range(PACK):
                 nc.tensor.matmul(
-                    v_turned[t][:, r, :], in_order[:, :, r], ident[:], start=(r == 0), stop=False, is_transpose=True
+                    v_turned[t][:, r, :], by_slot[:, :, r], ident[:], start=(r == 0), stop=False, is_transpose=True
                 )
-            if dealt:
-                return picked[t][:].rearrange("p (r h u) -> p h r u", r=PACK, h=H)
-            return picked[t][:].rearrange("p (h u r) -> p h u r", r=PACK, h=H)
 
-        def take_means(t, in_order, tag=None):
-            sums = held([P, H], F32, "sums%d" % t, tag)
-            nc.vector.tensor_reduce(sums[:], in_order, AX.XY, ALU.add)
+        def gather_on_vector(t, b):
+            picked = held([P, I], F32, "picked%d" % t)
+            by_slot = picked[:].rearrange("p (r s) -> p s r", r=PACK)
+            nc.vector.tensor_copy(by_slot, v_pool[t][:].indirect(offs_t[:]))
+            turn_values(t, by_slot, b)
+            return picked[:].rearrange("p (r h u) -> p h r u", r=PACK, h=H)
+
+        def gather_on_scalar(t, b):
+            picked = held([P, I], F32, "picked%d" % t)
+            nc.scalar.activation(picked[:], v_pool[t][:].indirect(offs_t[:]), ACT.Copy)
+            turn_values(t, picked[:].rearrange("p (s r) -> p s r", r=PACK), b)
+            return picked[:].rearrange("p (h u r) -> p h u r", r=PACK, h=H)
+
+        def stretch_sums(t, by_stretch):
+            sums = held([P, H], F32, "sums%d" % t)
+            nc.vector.tensor_reduce(sums[:], by_stretch, AX.XY, ALU.add)
+            return sums
+
+        def take_off_means(t, sums):
             neg_mean = held([P, H, STRETCH // PACK], F32, "neg_mean%d" % t)
             nc.vector.tensor_scalar(
                 neg_mean[:], sums[:].unsqueeze(2).to_broadcast([P, H, STRETCH // PACK]), -1.0 / STRETCH, None, ALU.mult
@@ -183,40 +180,37 @@ def tile_attend_answerodds_abstaining_centredvalues_pl_kernel(
                     start=False, stop=(r == PACK - 1), is_transpose=True,
                 )
 
-        def scale_values(t, tag=None):
-            v_bf = held([P, P, PACK], BF16, "v_bf%d" % t, tag)
+        def scale_values(t):
+            v_bf = held([P, P, PACK], BF16, "v_bf%d" % t)
             nc.vector.tensor_tensor(
-                v_bf[:], v_turned[t][:].rearrange("s r e -> s e r"),
+                v_bf[:], v_turned[t][:].rearrange("s r m -> s m r"),
                 vsc_t[:].unsqueeze(1).to_broadcast([P, P, PACK]), ALU.mult,
             )
-            return v_bf[:].rearrange("s e r -> s (e r)")
+            return v_bf[:].rearrange("s m r -> s (m r)")
 
         warm = held([P, 1], F32, "warm")
         nc.scalar.activation(warm[:], ones[:, 0:1], ACT.Sigmoid)
 
         thr_col = token_columns(token_row(thr_pool, "thr"), 2, "thr")
-
         kw = held([P, I], U16, "kw")
         nc.vector.tensor_copy(kw[:], kw_pool[:].indirect(offs_t[:]))
-
         steep_col = token_columns(token_row(steep_pool, "steep"), 3, "steep")
-
         ks = held([P, I], U8, "ks")
         nc.vector.tensor_copy(ks[:], ks_pool[:].indirect(offs_t[:]))
 
         q_bf = held([P, Q, PACK], BF16, "q_bf")
         nc.scalar.copy(
-            q_bf[:].rearrange("p (c i) j -> p c j i", i=PACK), q_raw[:].rearrange("p j (c i) -> p c j i", i=PACK)
+            q_bf[:].rearrange("p (c i) r -> p c r i", i=PACK), q_raw[:].rearrange("p r (c i) -> p c r i", i=PACK)
         )
 
-        steep_c = held([P, 4], F32, "steep_c")
-        shift_c = held([P, 4], F32, "shift_c")
+        steep_c = held([P, SLOT_TILES], F32, "steep_c")
+        shift_c = held([P, SLOT_TILES], F32, "shift_c")
         nc.vector.tensor_copy(steep_c[:], steep_col)
         nc.vector.scalar_tensor_tensor(shift_c[:], thr_col, -1.0, steep_c[:], ALU.mult, ALU.mult)
 
-        q_codes, q_scales = quantise(q_bf[:].rearrange("p q j -> p (q j)"), Q, "q")
+        q_codes, q_scales = quantise(q_bf[:].rearrange("p q r -> p (q r)"), Q, "q")
         a_ps = [bank([P, Q], b, "a_ps%d" % b) for b in (0, 1, 5, 7)]
-        for j in range(4):
+        for j in range(SLOT_TILES):
             nc.tensor.matmul_mx(
                 out=a_ps[j][:],
                 lhsT=kw[:, j * P : (j + 1) * P].bitcast(FP4X4),
@@ -226,59 +220,54 @@ def tile_attend_answerodds_abstaining_centredvalues_pl_kernel(
                 start=True,
                 stop=True,
             )
-
         guess_row = token_row(guess_pool, "guess")
+        picked0 = gather_on_vector(0, 6)
 
-        order0 = gather_values(0, False, 6, True)
-
-        sg = [held([P, Q], F32, "sg%d" % j) for j in range(4)]
-        for j in range(4):
+        sg = [held([P, Q], F32, "sg%d" % j) for j in range(SLOT_TILES)]
+        for j in range(SLOT_TILES):
             nc.scalar.activation(
                 sg[j][:], a_ps[j][:], ACT.Sigmoid, bias=shift_c[:, j : j + 1], scale=steep_c[:, j : j + 1]
             )
 
         guess_col = token_columns(guess_row, 0, "guess")
-
-        take_means(0, order0)
-
-        guess_c = held([P, 4], F32, "guess_c")
-        rest_c = held([P, 4], F32, "rest_c")
+        sums0 = stretch_sums(0, picked0)
+        guess_c = held([P, SLOT_TILES], F32, "guess_c")
+        rest_c = held([P, SLOT_TILES], F32, "rest_c")
         nc.vector.tensor_copy(guess_c[:], guess_col)
         nc.vector.tensor_scalar(rest_c[:], guess_col, -1.0, 1.0, ALU.mult, ALU.add)
-        chance = [held([P, Q], F32, "chance%d" % j) for j in range(4)]
-        for j in range(4):
+        take_off_means(0, sums0)
+
+        chance = [held([P, Q], F32, "chance%d" % j) for j in range(SLOT_TILES)]
+        for j in range(SLOT_TILES):
             nc.vector.tensor_scalar(
                 chance[j][:], sg[j][:], rest_c[:, j : j + 1], guess_c[:, j : j + 1], ALU.mult, ALU.add
             )
-        chance_q = [bank([P, I], b, "chance_q%d" % b) for b in (3, 4)]
+        chance_q = [bank([P, I], 3 + u, "chance_q%d" % u) for u in range(QT)]
         for u in range(QT):
-            for j in range(4):
+            for j in range(SLOT_TILES):
                 nc.tensor.transpose(chance_q[u][:, j * P : (j + 1) * P], chance[j][:, u * P : (u + 1) * P], ident[:])
-
-        order1 = gather_values(1, True, 7, False)
-
-        take_means(1, order1)
-
-        v_bf0 = scale_values(0)
-
-        os_all = bank([P, PACK, P], 6, "os_all")
-        for r in range(PACK):
-            nc.tensor.transpose(os_all[:, r, :], os_t[:, r : r + 1].to_broadcast([P, P]), ident[:])
-        w_mx = [None] * QT
-
-        ln_q = [held([P, I], F32, "ln_q%d" % u) for u in range(QT)]
-        ln_sum = [held([P, 1], F32, "ln_sum%d" % u) for u in range(QT)]
-        for u in range(QT):
-            nc.scalar.activation(ln_q[u][:], chance_q[u][:], ACT.Ln, accum_out=ln_sum[u][:])
-
-        order2 = gather_values(2, False, 5, True)
 
         neg_lam = held([P, QT], F32, "neg_lam")
         lam_mean = held([P, QT], F32, "lam_mean")
         nc.vector.tensor_scalar(neg_lam[:], lam_t[:], -1.0, None, ALU.mult)
         nc.vector.tensor_scalar(lam_mean[:], lam_t[:], 1.0 / I, None, ALU.mult)
 
-        v_mx[0] = quantise(v_bf0, P, "v0")
+        ln_q = [held([P, I], F32, "ln_q%d" % u) for u in range(QT)]
+        ln_sum = [held([P, 1], F32, "ln_sum%d" % u) for u in range(QT)]
+        for u in range(QT):
+            nc.scalar.activation(ln_q[u][:], chance_q[u][:], ACT.Ln, accum_out=ln_sum[u][:])
+        picked1 = gather_on_scalar(1, 3)
+        v_bf0 = scale_values(0)
+        sums1 = stretch_sums(1, picked1)
+        picked2 = gather_on_vector(2, 4)
+        take_off_means(1, sums1)
+        sums2 = stretch_sums(2, picked2)
+
+        take_off_means(2, sums2)
+
+        os_all = bank([P, PACK, P], 6, "os_all")
+        for r in range(PACK):
+            nc.tensor.transpose(os_all[:, r, :], os_t[:, r : r + 1].to_broadcast([P, P]), ident[:])
 
         neg_s = [held([P, I], F32, "neg_s%d" % u) for u in range(QT)]
         neg_m0 = [held([P, 1], F32, "neg_m0_%d" % u) for u in range(QT)]
@@ -287,109 +276,88 @@ def tile_attend_answerodds_abstaining_centredvalues_pl_kernel(
             nc.vector.tensor_scalar(
                 neg_s[u][:], ln_q[u][:], neg_lam[:, u : u + 1], None, ALU.mult, ALU.min, accum_out=neg_m0[u][:]
             )
+        v_mx0 = quantise(v_bf0, P, "v0")
         for u in range(QT):
             nc.vector.tensor_scalar(
                 lag[:, u : u + 1], ln_sum[u][:], lam_mean[:, u : u + 1], neg_m0[u][:], ALU.mult, ALU.add
             )
 
-        take_means(2, order2)
-
+        picked3 = gather_on_scalar(3, 1)
+        take_off_means(3, stretch_sums(3, picked3))
         v_bf1 = scale_values(1)
-
-        v_mx[1] = quantise(v_bf1, P, "v1")
-
-        order3 = gather_values(3, True, 1, False)
-
-        take_means(3, order3)
+        v_bf2 = scale_values(2)
 
         odds = held([P, QT], F32, "odds")
         for u in range(QT):
             nc.scalar.activation(
                 odds[:, u : u + 1], lag[:, u : u + 1], ACT.Exp, bias=thresh_t[:, u : u + 1], scale=eager_t[:, u : u + 1]
             )
-
-        p_t = [None] * QT
-        p_t[0] = held([P, I], F32, "p_t0")
-        p_sum0 = held([P, 1], F32, "p_sum0")
-        nc.scalar.activation(p_t[0][:], neg_s[0][:], ACT.Exp, bias=neg_m0[0][:], scale=-1.0, accum_out=p_sum0[:])
-        over0 = held([P, 1], F32, "over0")
-        nc.scalar.activation(over0[:], odds[:, 0 : 1], ACT.Identity, bias=p_sum0[:], scale=p_sum0[:])
-
-        p_t[1] = held([P, I], F32, "p_t1")
-        p_sum1 = held([P, 1], F32, "p_sum1")
-        nc.scalar.activation(p_t[1][:], neg_s[1][:], ACT.Exp, bias=neg_m0[1][:], scale=-1.0, accum_out=p_sum1[:])
-        over1 = held([P, 1], F32, "over1")
-        nc.scalar.activation(over1[:], odds[:, 1 : 2], ACT.Identity, bias=p_sum1[:], scale=p_sum1[:])
-
-        v_bf2 = scale_values(2)
-
-        share0 = held([P, 1], F32, "share0")
-        nc.vector.reciprocal(share0[:], over0[:])
-
-        share1 = held([P, 1], F32, "share1")
-        nc.vector.reciprocal(share1[:], over1[:])
-
-        w_q0 = held([P, P, PACK], BF16, "w_q0")
-        nc.vector.scalar_tensor_tensor(
-            w_q0[:], p_t[0][:].rearrange("q (s r) -> q s r", r=PACK), share0[:],
-            os_all[:].rearrange("q r s -> q s r"), ALU.mult, ALU.mult,
-        )
-        w_words0 = w_q0[:].rearrange("q s r -> q (s r)").bitcast(F32)
-        w_turned0 = bank([P, 2, P], 3, "w_turned0")
-        for h in range(2):
-            nc.tensor.transpose(w_turned0[:, h, :], w_words0[:, h : 2 * P : 2], ident[:])
-        w_bf0 = held([P, P, 2], F32, "w_bf0")
-        nc.scalar.copy(w_bf0[:], w_turned0[:].rearrange("s h q -> s q h"))
-
-        w_q1 = held([P, P, PACK], BF16, "w_q1")
-        nc.vector.scalar_tensor_tensor(
-            w_q1[:], p_t[1][:].rearrange("q (s r) -> q s r", r=PACK), share1[:],
-            os_all[:].rearrange("q r s -> q s r"), ALU.mult, ALU.mult,
-        )
-        w_words1 = w_q1[:].rearrange("q s r -> q (s r)").bitcast(F32)
-        w_turned1 = bank([P, 2, P], 4, "w_turned1")
-        for h in range(2):
-            nc.tensor.transpose(w_turned1[:, h, :], w_words1[:, h : 2 * P : 2], ident[:])
-        w_bf1 = held([P, P, 2], F32, "w_bf1")
-        nc.scalar.copy(w_bf1[:], w_turned1[:].rearrange("s h q -> s q h"))
-
-        v_mx[2] = quantise(v_bf2, P, "v2")
-
-        v_bf3 = scale_values(3)
-
-        w_mx[0] = quantise(w_bf0[:].rearrange("s q h -> s (q h)").bitcast(BF16), P, "w0")
-
-        v_mx[3] = quantise(v_bf3, P, "v3")
-
-        w_mx[1] = quantise(w_bf1[:].rearrange("s q h -> s (q h)").bitcast(BF16), P, "w1")
-
-        out_rows = out_0.rearrange("(p t) q -> p t q", t=PACK)
-        o_ps = [bank([P, PACK, P], 2 * u, "o_ps%d" % u) for u in range(QT)]
+        p = [held([P, I], F32, "p%d" % u) for u in range(QT)]
+        p_sum = [held([P, 1], F32, "p_sum%d" % u) for u in range(QT)]
+        over = [held([P, 1], F32, "over%d" % u) for u in range(QT)]
+        share = [held([P, 1], F32, "share%d" % u) for u in range(QT)]
         for u in range(QT):
-            for t in range(PACK):
+            nc.scalar.activation(p[u][:], neg_s[u][:], ACT.Exp, bias=neg_m0[u][:], scale=-1.0, accum_out=p_sum[u][:])
+            nc.scalar.activation(over[u][:], odds[:, u : u + 1], ACT.Identity, bias=p_sum[u][:], scale=p_sum[u][:])
+        for u in range(QT):
+            nc.vector.reciprocal(share[u][:], over[u][:])
+
+        def turned_weights(u):
+            w_q = held([P, P, PACK], BF16, "w_q%d" % u)
+            nc.vector.scalar_tensor_tensor(
+                w_q[:], p[u][:].rearrange("q (s r) -> q s r", r=PACK), share[u][:],
+                os_all[:].rearrange("q r s -> q s r"), ALU.mult, ALU.mult,
+            )
+            pairs = w_q[:].rearrange("q s r -> q (s r)").bitcast(F32)
+            w_turned = bank([P, 2, P], (7, 5)[u], "w_turned%d" % u)
+            for h in range(2):
+                nc.tensor.transpose(w_turned[:, h, :], pairs[:, h : 2 * P : 2], ident[:])
+            w_pairs = held([P, P, 2], F32, "w_pairs%d" % u)
+            nc.scalar.copy(w_pairs[:], w_turned[:].rearrange("s h q -> s q h"))
+            return w_pairs[:].rearrange("s q h -> s (q h)").bitcast(BF16)
+
+        w_bf = [turned_weights(u) for u in range(QT)]
+        v_mx1 = quantise(v_bf1, P, "v1")
+        v_bf3 = scale_values(3)
+        w_mx0 = quantise(w_bf[0], P, "w0")
+        v_mx2 = quantise(v_bf2, P, "v2")
+        v_mx3 = quantise(v_bf3, P, "v3")
+        w_mx1 = quantise(w_bf[1], P, "w1")
+
+        o_ps = [bank([P, PACK, P], 2 * u, "o_ps%d" % u) for u in range(QT)]
+        for u, (w_codes, w_scales) in enumerate((w_mx0, w_mx1)):
+            for t, (v_codes, v_scales) in enumerate((v_mx0, v_mx1, v_mx2, v_mx3)):
                 nc.tensor.matmul_mx(
                     out=o_ps[u][:, t, :],
-                    lhsT=v_mx[t][0][:].bitcast(FP8X4),
-                    lhsT_scale=v_mx[t][1][:],
-                    rhs=w_mx[u][0][:].bitcast(FP8X4),
-                    rhs_scale=w_mx[u][1][:],
+                    lhsT=v_codes[:].bitcast(FP8X4),
+                    lhsT_scale=v_scales[:],
+                    rhs=w_codes[:].bitcast(FP8X4),
+                    rhs_scale=w_scales[:],
                     start=True,
                     stop=True,
                 )
+
+        out_rows = out_0.rearrange("(p t) q -> p t q", t=PACK)
         o_sb = [held([P, PACK, P], F32, "o_sb%d" % u) for u in range(QT)]
         o_bf = [held([P, P, PACK], BF16, "o_bf%d" % u) for u in range(QT)]
         o_codes = held([P, Q], U32, "o_codes")
         o_scales = held([P, Q], U8, "o_scales")
+        halves = [slice(u * P, (u + 1) * P) for u in range(QT)]
+        nc.vector.tensor_copy(o_bf[0][:], o_ps[0][:].rearrange("p t q -> p q t"))
+        nc.scalar.copy(o_sb[1][:], o_ps[1][:])
+        nc.sync.dma_start(out_rows[:, :, halves[1]], o_sb[1][:])
+        nc.scalar.copy(o_sb[0][:], o_ps[0][:])
+        nc.scalar.dma_start(out_rows[:, :, halves[0]], o_sb[0][:])
+        nc.vector.tensor_copy(o_bf[1][:], o_sb[1][:].rearrange("p t q -> p q t"))
         for u in range(QT):
-            cols = slice(u * P, (u + 1) * P)
-            nc.vector.tensor_copy(o_bf[u][:], o_ps[u][:].rearrange("p t q -> p q t"))
-            nc.scalar.copy(o_sb[u][:], o_ps[u][:])
-            (nc.sync, nc.scalar)[u].dma_start(out_rows[:, :, cols], o_sb[u][:])
             nc.vector.quantize_mx(
-                out=o_codes[:, cols].bitcast(FP8X4), scales=o_scales[:, cols],
+                out=o_codes[:, halves[u]].bitcast(FP8X4), scales=o_scales[:, halves[u]],
                 in_=o_bf[u][:].rearrange("p q t -> p (q t)"),
             )
+
         nc.sync.dma_start(out_1[0].rearrange("p q r -> p (q r)").bitcast(I32), o_codes[:].bitcast(I32))
-        for g in range(4):
-            queue = nc.scalar if g == 3 else nc.sync
-            queue.dma_start(out_2[0, 4 * g : 4 * g + 4, :].bitcast(I32), o_scales[32 * g : 32 * g + 4, :].bitcast(I32))
+        for g in range(P // QUAD):
+            queue = nc.scalar if g == P // QUAD - 1 else nc.sync
+            queue.dma_start(
+                out_2[0, 4 * g : 4 * g + 4, :].bitcast(I32), o_scales[QUAD * g : QUAD * g + 4, :].bitcast(I32)
+            )

from contextlib import ExitStack

import concourse.mybir as mybir

D, T, I, Q, E = 512, 2048, 512, 256, 512
FLOPS = 2 * D * I * Q + 2 * I * E * Q

F32 = mybir.dt.float32
BF16 = mybir.dt.bfloat16
I32 = mybir.dt.int32
U32 = mybir.dt.uint32
U16 = mybir.dt.uint16
U8 = mybir.dt.uint8
FP8X4 = mybir.dt.float8_e4m3fn_x4
FP4X4 = mybir.dt.float4_e2m1fn_x4
ALU = mybir.AluOpType
ACT = mybir.ActivationFunctionType
AX = mybir.AxisListType

P = 128
PACK = 4
QUAD = 32
STRETCH = 16
H = I // STRETCH
SLOT_TILES = I // P
QT = Q // P
ROW = P - 1

TAKEOVERS = (
    ("ks_pool", 2048, (("steep_c", 0), ("q_codes", 128))),
    ("v_pool0", 8192, (("guess_c", 0), ("rest_c", 128))),
    ("sg3", 1024, (("neg_lam", 0), ("lam_mean", 128))),
    ("shift_c", 2048, (("picked1", 0),)),
    ("v_pool1", 8192, (("chance3", 0),)),
    ("v_pool2", 8192, (("neg_s0", 0), ("neg_s1", 2048), ("neg_mean1", 4096), ("v0_codes", 4608))),
    ("v_pool3", 8192, (("p0", 0), ("p1", 2048), ("odds", 4096), ("v_bf3", 0))),
)


def shared_offsets():
    offsets = {}
    start = 0
    for first, room, newcomers in TAKEOVERS:
        offsets[first] = start
        for name, at in newcomers:
            offsets[name] = start + at
        start = start + room
    return offsets


def tile_attend_answerodds_abstaining_centredvalues_pl_kernel(
    tc, query, keys_words, keys_scales, guess, steep, thr, lam, eager, thresh, slot_os, vals, vsc, offs,
    out_0, out_1, out_2,
):
    nc = tc.nc
    offsets = shared_offsets()
    with ExitStack() as ctx:
        sb = ctx.enter_context(tc.tile_pool(name="sb", bufs=1))
        shared = ctx.enter_context(tc.tile_pool(name="shared", bufs=1))
        ps = ctx.enter_context(tc.psum_pool(name="ps", bufs=1))

        def held(shape, dtype, name):
            if name in offsets:
                return shared.tile(shape, dtype, name=name, align_bytes=64, offset=offsets[name])
            return sb.tile(shape, dtype, name=name, align_bytes=64)

        def bank(shape, b, name):
            return ps.tile(shape, F32, name=name, tag="bank%d" % b)

        def quantise(bf, width, name):
            codes = held([P, width], U32, name + "_codes")
            scales = held([P, width], U8, name + "_scales")
            nc.vector.quantize_mx(out=codes[:].bitcast(FP8X4), scales=scales[:], in_=bf)
            return codes, scales

        offs_t = sb.tile([P, I // 16], U16, name="offs_t")
        kw_pool = held([P, T], U16, "kw_pool")
        ks_pool = held([P, T], U8, "ks_pool")
        thr_pool = held([P, T], F32, "thr_pool")
        steep_pool = held([P, T], F32, "steep_pool")
        guess_pool = held([P, T], F32, "guess_pool")
        q_raw = held([P, PACK, Q], F32, "q_raw")
        v_pool = [held([P, T], F32, "v_pool%d" % t) for t in range(PACK)]
        lam_t = held([P, QT], F32, "lam_t")
        eager_t = held([P, QT], F32, "eager_t")
        thresh_t = held([P, QT], F32, "thresh_t")
        os_t = held([P, PACK], F32, "os_t")
        vsc_t = held([P, PACK], F32, "vsc_t")

        ones = held([P, P], F32, "ones")
        quad_base = held([P, 1], F32, "quad_base")
        count = held([P, P], F32, "count")
        lane = held([P, QUAD], F32, "lane")
        ident = held([P, P], F32, "ident")
        nc.gpsimd.memset(ks_pool[:].bitcast(I32), 0)
        nc.gpsimd.memset(ones[:], 1.0)
        for g in range(P // QUAD):
            nc.gpsimd.memset(quad_base[QUAD * g : QUAD * (g + 1), :], float(QUAD * g))
        nc.vector.memset(thr_pool[0:ROW, :].bitcast(I32), 0)
        nc.vector.tensor_tensor_scan(count[:], ones[:], ones[:], 0.0, ALU.mult, ALU.add)
        nc.vector.memset(steep_pool[0:ROW, :].bitcast(I32), 0)
        nc.vector.transpose(lane[:], count[:, 0:QUAD])
        nc.vector.memset(guess_pool[0:ROW, :].bitcast(I32), 0)
        nc.vector.tensor_scalar(ident[:], count[:], quad_base[:], lane[:, 0:1], ALU.subtract, ALU.is_equal)

        def load_by_query(dst, src):
            with nc.allow_non_contiguous_dma(reason="one number a query row"):
                nc.sync.dma_start(dst[:], src[:, 0].rearrange("(u p) -> p u", p=P))

        def load_by_slot(dst, src):
            nc.sync.dma_start(dst[:], src[0].rearrange("(s r) -> s r", r=PACK))

        v_rows = vals.rearrange("(p t) n -> t p n", t=PACK)
        nc.sync.dma_start(offs_t[:], offs)
        nc.scalar.dma_start(thr_pool[ROW:P, :], thr[0:1, :])
        nc.scalar.dma_start(steep_pool[ROW:P, :], steep[0:1, :])
        nc.sync.dma_start(guess_pool[ROW:P, :], guess[0:1, :])
        nc.sync.dma_start(kw_pool[:].bitcast(I32), keys_words[0].bitcast(I32))
        nc.sync.dma_start(q_raw[:], query.rearrange("(p r) q -> p r q", r=PACK))
        for g in range(P // QUAD):
            nc.sync.dma_start(
                ks_pool[QUAD * g : QUAD * g + 4, :].bitcast(I32), keys_scales[0, 4 * g : 4 * g + 4, :].bitcast(I32)
            )
        nc.sync.dma_start(v_pool[0][:], v_rows[0])
        load_by_slot(vsc_t, vsc)
        nc.sync.dma_start(v_pool[1][:], v_rows[1])
        load_by_query(lam_t, lam)
        nc.sync.dma_start(v_pool[2][:], v_rows[2])
        nc.sync.dma_start(v_pool[3][:], v_rows[3])
        load_by_slot(os_t, slot_os)
        load_by_query(eager_t, eager)
        load_by_query(thresh_t, thresh)

        def token_row(pool, name):
            row = held([P, I], F32, name + "_row")
            nc.scalar.activation(row[:], pool[:].indirect(offs_t[:]), ACT.Copy)
            return row

        def token_columns(row, b, name):
            turned = bank([P, SLOT_TILES, P], b, name + "_turned")
            for j in range(SLOT_TILES):
                nc.tensor.transpose(turned[:, j, :], row[:, j * P : (j + 1) * P], ident[:])
            return turned[:, :, ROW]

        v_turned = [None] * PACK

        def turn_values(t, by_slot, b):
            v_turned[t] = bank([P, PACK, P], b, "v_turned%d" % t)
            for r in range(PACK):
                nc.tensor.matmul(
                    v_turned[t][:, r, :], by_slot[:, :, r], ident[:], start=(r == 0), stop=False, is_transpose=True
                )

        def gather_on_vector(t, b):
            picked = held([P, I], F32, "picked%d" % t)
            by_slot = picked[:].rearrange("p (r s) -> p s r", r=PACK)
            nc.vector.tensor_copy(by_slot, v_pool[t][:].indirect(offs_t[:]))
            turn_values(t, by_slot, b)
            return picked[:].rearrange("p (r h u) -> p h r u", r=PACK, h=H)

        def gather_on_scalar(t, b):
            picked = held([P, I], F32, "picked%d" % t)
            nc.scalar.activation(picked[:], v_pool[t][:].indirect(offs_t[:]), ACT.Copy)
            turn_values(t, picked[:].rearrange("p (s r) -> p s r", r=PACK), b)
            return picked[:].rearrange("p (h u r) -> p h u r", r=PACK, h=H)

        def stretch_sums(t, by_stretch):
            sums = held([P, H], F32, "sums%d" % t)
            nc.vector.tensor_reduce(sums[:], by_stretch, AX.XY, ALU.add)
            return sums

        def take_off_means(t, sums):
            neg_mean = held([P, H, STRETCH // PACK], F32, "neg_mean%d" % t)
            nc.vector.tensor_scalar(
                neg_mean[:], sums[:].unsqueeze(2).to_broadcast([P, H, STRETCH // PACK]), -1.0 / STRETCH, None, ALU.mult
            )
            for r in range(PACK):
                nc.tensor.matmul(
                    v_turned[t][:, r, :], neg_mean[:].rearrange("p h u -> p (h u)"), ident[:],
                    start=False, stop=(r == PACK - 1), is_transpose=True,
                )

        def scale_values(t):
            v_bf = held([P, P, PACK], BF16, "v_bf%d" % t)
            nc.vector.tensor_tensor(
                v_bf[:], v_turned[t][:].rearrange("s r m -> s m r"),
                vsc_t[:].unsqueeze(1).to_broadcast([P, P, PACK]), ALU.mult,
            )
            return v_bf[:].rearrange("s m r -> s (m r)")

        warm = held([P, 1], F32, "warm")
        nc.scalar.activation(warm[:], ones[:, 0:1], ACT.Sigmoid)

        thr_col = token_columns(token_row(thr_pool, "thr"), 2, "thr")
        kw = held([P, I], U16, "kw")
        nc.vector.tensor_copy(kw[:], kw_pool[:].indirect(offs_t[:]))
        steep_col = token_columns(token_row(steep_pool, "steep"), 3, "steep")
        ks = held([P, I], U8, "ks")
        nc.vector.tensor_copy(ks[:], ks_pool[:].indirect(offs_t[:]))

        q_bf = held([P, Q, PACK], BF16, "q_bf")
        nc.scalar.copy(
            q_bf[:].rearrange("p (c i) r -> p c r i", i=PACK), q_raw[:].rearrange("p r (c i) -> p c r i", i=PACK)
        )

        steep_c = held([P, SLOT_TILES], F32, "steep_c")
        shift_c = held([P, SLOT_TILES], F32, "shift_c")
        nc.vector.tensor_copy(steep_c[:], steep_col)
        nc.vector.scalar_tensor_tensor(shift_c[:], thr_col, -1.0, steep_c[:], ALU.mult, ALU.mult)

        q_codes, q_scales = quantise(q_bf[:].rearrange("p q r -> p (q r)"), Q, "q")
        a_ps = [bank([P, Q], b, "a_ps%d" % b) for b in (0, 1, 5, 7)]
        for j in range(SLOT_TILES):
            nc.tensor.matmul_mx(
                out=a_ps[j][:],
                lhsT=kw[:, j * P : (j + 1) * P].bitcast(FP4X4),
                lhsT_scale=ks[:, j * P : (j + 1) * P],
                rhs=q_codes[:].bitcast(FP8X4),
                rhs_scale=q_scales[:],
                start=True,
                stop=True,
            )
        guess_row = token_row(guess_pool, "guess")
        picked0 = gather_on_vector(0, 6)

        sg = [held([P, Q], F32, "sg%d" % j) for j in range(SLOT_TILES)]
        for j in range(SLOT_TILES):
            nc.scalar.activation(
                sg[j][:], a_ps[j][:], ACT.Sigmoid, bias=shift_c[:, j : j + 1], scale=steep_c[:, j : j + 1]
            )

        guess_col = token_columns(guess_row, 0, "guess")
        sums0 = stretch_sums(0, picked0)
        guess_c = held([P, SLOT_TILES], F32, "guess_c")
        rest_c = held([P, SLOT_TILES], F32, "rest_c")
        nc.vector.tensor_copy(guess_c[:], guess_col)
        nc.vector.tensor_scalar(rest_c[:], guess_col, -1.0, 1.0, ALU.mult, ALU.add)
        take_off_means(0, sums0)

        chance = [held([P, Q], F32, "chance%d" % j) for j in range(SLOT_TILES)]
        for j in range(SLOT_TILES):
            nc.vector.tensor_scalar(
                chance[j][:], sg[j][:], rest_c[:, j : j + 1], guess_c[:, j : j + 1], ALU.mult, ALU.add
            )
        chance_q = [bank([P, I], 3 + u, "chance_q%d" % u) for u in range(QT)]
        for u in range(QT):
            for j in range(SLOT_TILES):
                nc.tensor.transpose(chance_q[u][:, j * P : (j + 1) * P], chance[j][:, u * P : (u + 1) * P], ident[:])

        neg_lam = held([P, QT], F32, "neg_lam")
        lam_mean = held([P, QT], F32, "lam_mean")
        nc.vector.tensor_scalar(neg_lam[:], lam_t[:], -1.0, None, ALU.mult)
        nc.vector.tensor_scalar(lam_mean[:], lam_t[:], 1.0 / I, None, ALU.mult)

        ln_q = [held([P, I], F32, "ln_q%d" % u) for u in range(QT)]
        ln_sum = [held([P, 1], F32, "ln_sum%d" % u) for u in range(QT)]
        for u in range(QT):
            nc.scalar.activation(ln_q[u][:], chance_q[u][:], ACT.Ln, accum_out=ln_sum[u][:])
        picked1 = gather_on_scalar(1, 3)
        v_bf0 = scale_values(0)
        sums1 = stretch_sums(1, picked1)
        picked2 = gather_on_vector(2, 4)
        take_off_means(1, sums1)
        sums2 = stretch_sums(2, picked2)

        take_off_means(2, sums2)

        os_all = bank([P, PACK, P], 6, "os_all")
        for r in range(PACK):
            nc.tensor.transpose(os_all[:, r, :], os_t[:, r : r + 1].to_broadcast([P, P]), ident[:])

        neg_s = [held([P, I], F32, "neg_s%d" % u) for u in range(QT)]
        neg_m0 = [held([P, 1], F32, "neg_m0_%d" % u) for u in range(QT)]
        lag = held([P, QT], F32, "lag")
        for u in range(QT):
            nc.vector.tensor_scalar(
                neg_s[u][:], ln_q[u][:], neg_lam[:, u : u + 1], None, ALU.mult, ALU.min, accum_out=neg_m0[u][:]
            )
        v_mx0 = quantise(v_bf0, P, "v0")
        for u in range(QT):
            nc.vector.tensor_scalar(
                lag[:, u : u + 1], ln_sum[u][:], lam_mean[:, u : u + 1], neg_m0[u][:], ALU.mult, ALU.add
            )

        picked3 = gather_on_scalar(3, 1)
        take_off_means(3, stretch_sums(3, picked3))
        v_bf1 = scale_values(1)
        v_bf2 = scale_values(2)

        odds = held([P, QT], F32, "odds")
        for u in range(QT):
            nc.scalar.activation(
                odds[:, u : u + 1], lag[:, u : u + 1], ACT.Exp, bias=thresh_t[:, u : u + 1], scale=eager_t[:, u : u + 1]
            )
        p = [held([P, I], F32, "p%d" % u) for u in range(QT)]
        p_sum = [held([P, 1], F32, "p_sum%d" % u) for u in range(QT)]
        over = [held([P, 1], F32, "over%d" % u) for u in range(QT)]
        share = [held([P, 1], F32, "share%d" % u) for u in range(QT)]
        for u in range(QT):
            nc.scalar.activation(p[u][:], neg_s[u][:], ACT.Exp, bias=neg_m0[u][:], scale=-1.0, accum_out=p_sum[u][:])
            nc.scalar.activation(over[u][:], odds[:, u : u + 1], ACT.Identity, bias=p_sum[u][:], scale=p_sum[u][:])
        for u in range(QT):
            nc.vector.reciprocal(share[u][:], over[u][:])

        def turned_weights(u):
            w_q = held([P, P, PACK], BF16, "w_q%d" % u)
            nc.vector.scalar_tensor_tensor(
                w_q[:], p[u][:].rearrange("q (s r) -> q s r", r=PACK), share[u][:],
                os_all[:].rearrange("q r s -> q s r"), ALU.mult, ALU.mult,
            )
            pairs = w_q[:].rearrange("q s r -> q (s r)").bitcast(F32)
            w_turned = bank([P, 2, P], (7, 5)[u], "w_turned%d" % u)
            for h in range(2):
                nc.tensor.transpose(w_turned[:, h, :], pairs[:, h : 2 * P : 2], ident[:])
            w_pairs = held([P, P, 2], F32, "w_pairs%d" % u)
            nc.scalar.copy(w_pairs[:], w_turned[:].rearrange("s h q -> s q h"))
            return w_pairs[:].rearrange("s q h -> s (q h)").bitcast(BF16)

        w_bf = [turned_weights(u) for u in range(QT)]
        v_mx1 = quantise(v_bf1, P, "v1")
        v_bf3 = scale_values(3)
        w_mx0 = quantise(w_bf[0], P, "w0")
        v_mx2 = quantise(v_bf2, P, "v2")
        v_mx3 = quantise(v_bf3, P, "v3")
        w_mx1 = quantise(w_bf[1], P, "w1")

        o_ps = [bank([P, PACK, P], 2 * u, "o_ps%d" % u) for u in range(QT)]
        for u, (w_codes, w_scales) in enumerate((w_mx0, w_mx1)):
            for t, (v_codes, v_scales) in enumerate((v_mx0, v_mx1, v_mx2, v_mx3)):
                nc.tensor.matmul_mx(
                    out=o_ps[u][:, t, :],
                    lhsT=v_codes[:].bitcast(FP8X4),
                    lhsT_scale=v_scales[:],
                    rhs=w_codes[:].bitcast(FP8X4),
                    rhs_scale=w_scales[:],
                    start=True,
                    stop=True,
                )

        out_rows = out_0.rearrange("(p t) q -> p t q", t=PACK)
        o_sb = [held([P, PACK, P], F32, "o_sb%d" % u) for u in range(QT)]
        o_bf = [held([P, P, PACK], BF16, "o_bf%d" % u) for u in range(QT)]
        o_codes = held([P, Q], U32, "o_codes")
        o_scales = held([P, Q], U8, "o_scales")
        halves = [slice(u * P, (u + 1) * P) for u in range(QT)]
        nc.vector.tensor_copy(o_bf[0][:], o_ps[0][:].rearrange("p t q -> p q t"))
        nc.scalar.copy(o_sb[1][:], o_ps[1][:])
        nc.sync.dma_start(out_rows[:, :, halves[1]], o_sb[1][:])
        nc.scalar.copy(o_sb[0][:], o_ps[0][:])
        nc.scalar.dma_start(out_rows[:, :, halves[0]], o_sb[0][:])
        nc.vector.tensor_copy(o_bf[1][:], o_sb[1][:].rearrange("p t q -> p q t"))
        for u in range(QT):
            nc.vector.quantize_mx(
                out=o_codes[:, halves[u]].bitcast(FP8X4), scales=o_scales[:, halves[u]],
                in_=o_bf[u][:].rearrange("p q t -> p (q t)"),
            )

        nc.sync.dma_start(out_1[0].rearrange("p q r -> p (q r)").bitcast(I32), o_codes[:].bitcast(I32))
        for g in range(P // QUAD):
            queue = nc.scalar if g == P // QUAD - 1 else nc.sync
            queue.dma_start(
                out_2[0, 4 * g : 4 * g + 4, :].bitcast(I32), o_scales[QUAD * g : QUAD * g + 4, :].bitcast(I32)
            )
